import numpy as np, ml_dtypes
CORES = [3,11,19,27,35,43,51,59]
N = 8
BF = ml_dtypes.bfloat16
def gentries(a):
    return np.ascontiguousarray(a.reshape(8, 16, -1).transpose(0, 2, 1)).reshape(8, -1)
def gtable(e):
    e = np.asarray(e); return np.ascontiguousarray(e.reshape(8, -1, 16).transpose(0, 2, 1)).reshape(128, -1).astype(np.int32)
S, Q, STEPS = 4096, 96, 1
def whole(rng, *shape):
    return rng.integers(-7, 8, shape).astype(np.float32).astype(BF)
def neighbours(rng, nb):
    own = np.arange(S); nb = np.where(rng.random((N, 8, 1, S)) < 0.0625, own, nb); nb[:, :, 0] = own
    return nb.reshape(N, 128, S).astype(np.int32)
def lists(e):
    return np.stack([gtable(x) for x in e])
def setup_inputs(rng):
    return {"k": whole(rng, N, 128, S), "nb": neighbours(rng, rng.integers(0, S, (N, 8, 16, S))), "br": rng.integers(0, S, (N, 8, S)).astype(np.int32),
            "q": whole(rng, N, 128, Q), "entry": lists(rng.integers(0, S, (N, 8, Q)))}
def setup_inputs_ties(rng):
    d = setup_inputs(rng); q = np.zeros((N, 8, 16, Q), np.float32)
    for i in range(2): np.put_along_axis(q, rng.integers(0, 16, (N, 8, 1, Q)), rng.choice(np.array([-1, 1], np.float32), (N, 8, 1, Q)), 2)
    q[:, :, :, 3] = 0; d["q"] = q.reshape(N, 128, Q).astype(BF)
    nb = d["nb"].reshape(N, 8, 16, S).copy(); nb[:, :, 9:] = np.where(rng.random((N, 8, 1, S)) < 0.25, nb[:, :, 1:8], nb[:, :, 9:])
    d["nb"] = nb.reshape(N, 128, S); return d
def setup_inputs_ends(rng):
    d = setup_inputs(rng); z = np.array([0, 1, S - 2, S - 1])
    nb = d["nb"].reshape(N, 8, 16, S); nb = np.where(rng.random(nb.shape) < 0.5, z[rng.integers(0, 4, nb.shape)], nb); nb[:, :, 0] = np.arange(S); nb[:, :, :, S - 2] = S - 2
    br = d["br"]; d["br"] = np.where(rng.random(br.shape) < 0.5, z[rng.integers(0, 4, br.shape)], br).astype(np.int32)
    e = z[rng.integers(0, 4, (N, 8, Q))]; e[:, :, 0] = S - 1; e[:, :, 1] = S - 2; d["entry"] = lists(e)
    q = d["q"].astype(np.float32).reshape(N, 8, 16, Q); q[:, :, :, :2] = 7 * rng.choice(np.array([-1, 1], np.float32), (N, 8, 16, 2))
    k = d["k"].astype(np.float32).reshape(N, 8, 16, S); k[:, :, :, S - 1] = q[:, :, :, 0]; k[:, :, :, S - 2] = -q[:, :, :, 1]
    d["nb"] = nb.reshape(N, 128, S).astype(np.int32); d["q"] = q.reshape(N, 128, Q).astype(BF); d["k"] = k.reshape(N, 128, S).astype(BF); return d
def setup_inputs_one(rng):
    d = setup_inputs(rng); e = rng.integers(0, S, (N, 8, 1)); b = rng.integers(0, S, (N, 8, 1))
    d["entry"] = lists(np.repeat(e, Q, axis=2)); d["br"] = np.repeat(b, S, axis=2).astype(np.int32); return d
def setup_inputs_spread(rng):
    d = setup_inputs(rng)
    for a in ("k", "q"):
        z = rng.choice(np.array([0, 1, 2, 3, 5, 7, 7, 7]), (N, 8, 1, d[a].shape[-1])); d[a] = rng.integers(-z, z + 1, (N, 8, 16, d[a].shape[-1])).reshape(d[a].shape).astype(np.float32).astype(BF)
    low = lambda *shape: np.minimum(np.floor(S * rng.random(shape) ** 4), S - 1).astype(np.int64)
    nb = neighbours(rng, low(N, 8, 16, S)).reshape(N, 8, 16, S); nb[:, :, 2:] = np.where(rng.random((N, 8, 1, S)) < 0.25, nb[:, :, 1:2], nb[:, :, 2:])
    d["nb"] = nb.reshape(N, 128, S); d["br"] = low(N, 8, S).astype(np.int32); d["entry"] = lists(low(N, 8, Q)); return d
def check_inputs(d):
    bad = []
    for a in ("k", "q"):
        x = d[a].astype(np.float32)
        if not ((np.abs(x) <= 7) & (np.rint(x) == x)).all(): bad.append(a + "_whole")
    for a in ("nb", "br", "entry"):
        if not ((d[a] >= 0) & (d[a] < S)).all(): bad.append(a + "_range")
    if not (d["nb"][:, ::16] == np.arange(S)).all(): bad.append("nb_self")
    return bad
def reference(k, nb, br, q, entry):
    y = np.zeros((N, 8, 16, Q), np.int64); gr = np.arange(8)[:, None, None, None]; ft = np.arange(16)[None, :, None, None]
    keys = k.astype(np.float32).astype(np.int32).reshape(N, 8, 16, S); vals = k.astype(np.float32).astype(np.int32).reshape(N, 8, 16, S)
    nbs = nb.reshape(N, 8, 16, S); qs = q.astype(np.float32).astype(np.int32).reshape(N, 8, 16, Q)
    for r in range(N):
        at = gentries(entry[r])
        for s in range(N):
            t = (r + s) % N
            for step in range(STEPS):
                c = np.take_along_axis(nbs[t], at[:, None], 2)
                score = np.sum(keys[t][gr, ft, c[:, None]] * qs[r][:, :, None], axis=1)
                p = np.argmax(score, axis=1)[:, None]
                at = np.take_along_axis(c, p, 1)[:, 0]; best = np.take_along_axis(score, p, 1)
            y[r] += np.maximum(best, 0) * np.take_along_axis(vals[t], at[:, None], 2)
            at = np.take_along_axis(br[t], at, 1)
    return {"y": y.reshape(N, 128, Q).astype(np.float32)}

@@ -1,0 +1,396 @@
+from concourse.bass import DstId, RemoteDMATransfer
+from concourse.mybir import AluOpType as A, ActivationFunctionType as F
+
+N, S, Q = 8, 4096, 96
+H = Q // 2
+B = H // 16
+NW = 2 * N
+CHUNKS = ((0, 8), (8, 14), (14, 16))
+PART1 = 128
+SCALAR_BRIDGE = True
+SCALE = 4096.0
+BIG = 1.0e9
+
+SCRATCH = {
+    "nbI": ("sbuf", [128, S], "int32"),
+    "kS": ("sbuf", [128, S], "bfloat16"),
+    "nbbr": ("sbuf", [128, S], "float32"),
+    "qall": ("sbuf", [128, N * Q], "bfloat16"),
+    "qrep": ("sbuf", [128, NW * 16 * H], "bfloat16"),
+    "prod": ("sbuf", [128, NW * 16 * H], "bfloat16"),
+    "brX": ("sbuf", [128, 256], "int32"),
+    "brT": ("sbuf", [128, 8, 2, 16], "float32"),
+    "brY": ("sbuf", [128, 256], "uint16"),
+    "brIn": ("sbuf", [128, 256], "uint16"),
+    "ent": ("sbuf", [128, 8], "int32"),
+    "lin": ("sbuf", [128, NW * 8], "uint16"),
+    "lout": ("sbuf", [128, NW * 8], "uint16"),
+    "cu": ("sbuf", [128, NW * H], "uint16"),
+    "cf": ("sbuf", [128, NW * H], "float32"),
+    "dup": ("sbuf", [128, NW * 2 * H], "float32"),
+    "dupT": ("sbuf", [128, NW * B, 2, 16], "float32"),
+    "rmax": ("sbuf", [128, NW * H], "float32"),
+    "dd": ("sbuf", [128, NW * H], "float32"),
+    "ee": ("sbuf", [128, NW * H], "float32"),
+    "sel": ("sbuf", [128, NW * H], "float32"),
+    "rr": ("sbuf", [128, NW * H], "float32"),
+    "srep": ("sbuf", [128, NW * H], "float32"),
+    "term": ("sbuf", [128, NW * H], "float32"),
+    "termN": ("sbuf", [128, NW * H], "float32"),
+    "accin": ("sbuf", [128, (N + 1) * Q], "float32"),
+    "rmask": ("sbuf", [128, H], "float32"),
+    "ebig": ("sbuf", [128, 144], "bfloat16"),
+    "iI": ("sbuf", [128, H], "int32"),
+    "iP": ("sbuf", [128, 16], "int32"),
+    "iD": ("sbuf", [128, 160], "int32"),
+    "iB": ("sbuf", [128, 128], "int32"),
+    "iJ": ("sbuf", [128, 32], "int32"),
+    "iS": ("sbuf", [128, 8], "int32"),
+    "t16": ("sbuf", [128, 16], "int32"),
+    "evI": ("sbuf", [128, 4], "int32"),
+    "cols": ("sbuf", [128, 16], "float32"),
+    "m16": ("sbuf", [128, 16], "float32"),
+    "mE": ("sbuf", [128, 160], "float32"),
+    "mO": ("sbuf", [128, 160], "float32"),
+    "boI": ("sbuf", [128, 128], "int32"),
+    "bo": ("sbuf", [128, 128], "float32"),
+    "q0off": ("sbuf", [128, H], "uint16"),
+    "s2off": ("sbuf", [128, 8], "uint16"),
+    "jj": ("sbuf", [128, 32], "float32"),
+    "j47": ("sbuf", [128, 32], "float32"),
+    "brF": ("sbuf", [128, 256], "float32"),
+    "pX": ("sbuf", [128, 416], "float32"),
+    "pK": ("sbuf", [128, 416], "float32"),
+    "pKi": ("sbuf", [128, 416], "int32"),
+    "pR": ("sbuf", [128, 416], "float32"),
+    "poff": ("sbuf", [128, 416], "uint16"),
+    "pU0": ("psum", [128, 512], "float32"), "pU1": ("psum", [128, 512], "float32"),
+    "pP0": ("psum", [128, 512], "float32"), "pP1": ("psum", [128, 512], "float32"),
+    "pS0": ("psum", [128, 512], "float32"), "pS1": ("psum", [128, 512], "float32"),
+    "pB": ("psum", [128, 512], "float32"),
+}
+ROLES = ["v1", "vf", "v2a", "v2b", "v2c", "vtr", "v3", "v4", "v5", "v6", "v7", "v8", "s1", "s2", "sr", "sc", "su", "pu", "pp", "ps"]
+SEMAPHORES = (["ldq", "ldbr", "lden", "ldnb", "ldk", "g1", "g2", "g3", "vs", "vq0", "vI", "vX", "vC", "vY", "vq", "vnb", "pb", "kgo",
+               "loc", "arY", "arH", "st", "fin0", "fin1"]
+              + ["%s_%d" % (r, w) for r in ROLES for w in range(2)]
+              + ["sq%d" % n for n in range(NW)] + ["arl%d" % n for n in range(2, NW)]
+              + ["ara%d" % s for s in range(1, N)] + ["arq%d" % s for s in range(1, N)])
+
+
+def helper_of(core, cores, topo):
+    ok = [c for c in topo.cores_of(core) if c not in cores and all(topo.may_write(c, d) for d in cores)]
+    same = [c for c in ok if topo.die(c) == topo.die(core)]
+    return (same or ok)[0]
+
+
+def bits(m):
+    return bin(m).count("1")
+
+
+def helper_program(g, core, owner, T, topo):
+    sem = T.sem
+    oc = T.cores[owner]
+    nxt = T.cores[(owner + 1) % N]
+    g.wait_ge(sem["arH"], bits(topo.mask(oc, core) & topo.mask(oc, nxt)))
+    total = 0
+    for s in range(2, N):
+        d = T.cores[(owner + s) % N]
+        rid, pid, _ = topo.addr(d)
+        m = topo.mask(core, d)
+        g.remote_dma(T.qall[:, s * Q:(s + 1) * Q], T.qall[:, 0:Q], sem["arq%d" % s], sem["loc"], pid, rid, m)
+        total += bits(m)
+    g.wait_ge(sem["loc"], total)
+
+
+def rank_program(g, core, T, topo):
+    cores = list(T.cores)
+    rank = T.rank_of(core)
+    if rank is None:
+        for r, c in enumerate(cores):
+            if helper_of(c, cores, topo) == core:
+                helper_program(g, core, r, T, topo)
+        return
+    sem = T.sem
+    V, SC, PE, SY = g.vector, g.scalar, g.tensor, g.sync
+    nxt, prv = cores[(rank + 1) % N], cores[(rank - 1) % N]
+    nrid, npid, _ = topo.addr(nxt)
+    nmask = topo.mask(core, nxt)
+    nin = bits(topo.mask(prv, core))
+    hlp = helper_of(core, cores, topo)
+    loc = [0]
+
+    def sm(role, w):
+        return sem["%s_%d" % (role, w)]
+
+    def wv(buf, n):
+        return buf[:, n * H:(n + 1) * H]
+
+    SY.dma_start(T.brX[:], T.br[:]).then_inc(sem.ldbr, 16)
+    SC.dma_start(T.qall[:, 0:Q], T.q[:]).then_inc(sem.ldq, 16)
+    SC.dma_start(T.ent[:, 0:6], T.entry[:]).then_inc(sem.lden, 16)
+    SY.dma_start(T.nbI[:], T.nb[:]).then_inc(sem.ldnb, 16)
+    SY.wait_ge(sem.kgo, 1)
+    SY.dma_start(T.kS[:], T.k[:]).then_inc(sem.ldk, 16)
+
+    g.iota(T.iP[:], [[-1, 16]], 16, 1).then_inc(sem.g2, 1)
+    g.iota(T.iD[:], [[-1, 160]], 16, 1).then_inc(sem.g2, 1)
+    g.iota(T.iI[:], [[1, H]], 0, 0).then_inc(sem.g1, 1)
+    g.iota(T.iB[:], [[-16, 8], [0, 16]], 0, 1).then_inc(sem.g3, 1)
+    g.iota(T.iJ[:], [[0, 8], [16, 4]], 0, 0).then_inc(sem.g3, 1)
+    g.iota(T.iS[:], [[1, 4], [0, 2]], 0, 0).then_inc(sem.g3, 1)
+
+    def send(dst, src, rsem):
+        g.remote_dma(dst, src, rsem, sem.loc, npid, nrid, nmask)
+        loc[0] += bits(nmask)
+
+    def send_sum(dst, srcs, rsem):
+        g.remote_dma_fused([RemoteDMATransfer(dst_ids=[DstId(rid=nrid, pnc=npid)], dma_engine_mask=nmask, remote_sem=rsem,
+                                              srcs=srcs, dsts=[dst], alu_op=1)], local_sem=sem.loc)
+        loc[0] += bits(nmask)
+
+    g.wait_ge(sem.ldq, 16)
+    send(T.qall[:, Q:2 * Q], T.qall[:, 0:Q], sem.arq1)
+    hrid, hpid, _ = topo.addr(hlp)
+    hmask = topo.mask(core, hlp) & nmask
+    g.remote_dma(T.qall[:, 0:Q], T.qall[:, 0:Q], sem.arH, sem.loc, hpid, hrid, hmask)
+    loc[0] += bits(hmask)
+    g.wait_ge(sem.vY, 16)
+    send(T.brIn[:], T.brY[:], sem.arY)
+    g.sem_inc(sem.kgo, 1)
+
+    def send_acc(s):
+        g.wait_ge(sm("su", 0), s + 1)
+        g.wait_ge(sm("su", 1), s + 1)
+        dst = T.accin[:, (s + 1) * Q:(s + 2) * Q]
+        src = T.termN[:, s * Q:(s + 1) * Q]
+        if s == 0:
+            send(dst, src, sem["ara1"])
+        else:
+            g.wait_ge(sem["ara%d" % s], nin)
+            send_sum(dst, [src, T.accin[:, s * Q:(s + 1) * Q]], sem["ara%d" % (s + 1)])
+
+    for n in range(NW):
+        s, w = divmod(n, 2)
+        if s < N - 1:
+            g.wait_ge(sm("v7", w), s + 1)
+            send(T.lin[:, 8 * (n + 2):8 * (n + 2) + 4], T.lout[:, 8 * n:8 * n + 4], sem["arl%d" % (n + 2)])
+        if w == 0 and s >= 1:
+            send_acc(s - 1)
+    g.wait_ge(sem["ara%d" % (N - 1)], nin)
+    for w in range(2):
+        n = NW - 2 + w
+        g.wait_ge(sm("su", w), N)
+        send_sum(wv(T.accin, n + 2), [wv(T.termN, n), wv(T.accin, n)], sem["fin%d" % w])
+    g.wait_ge(sem.loc, loc[0])
+
+    for w in range(2):
+        SY.wait_ge(sem["fin%d" % w], nin)
+        SY.dma_start(T.y[:, w * H:(w + 1) * H], wv(T.accin, NW + w)).then_inc(sem.st, 16)
+    SY.wait_ge(sem.st, 32)
+
+    vs = [0]
+
+    def v(ins):
+        ins.then_inc(sem.vs, 1)
+        vs[0] += 1
+
+    def vw():
+        V.wait_ge(sem.vs, vs[0])
+
+    even, odd, pm, pm3 = T.cols[:, 0:1], T.cols[:, 4:5], T.cols[:, 8:9], T.cols[:, 12:13]
+    v(V.memset(T.rmask[:], 0.0))
+    v(V.memset(T.ebig[:], 0.0))
+    v(V.memset(T.lout[:], 0))
+    V.wait_ge(sem.g2, 2)
+    v(V.tensor_scalar(T.t16[:], T.iP[:], 15, None, A.bitwise_and))
+    v(V.tensor_scalar(T.evI[:, 0:1], T.iP[:, 0:1], 4, 1, A.arith_shift_right, A.bitwise_and))
+    vw()
+    v(V.tensor_copy(even, T.evI[:, 0:1]))
+    v(V.tensor_scalar(odd, T.evI[:, 0:1], -1.0, 1.0, A.mult, A.add))
+    v(V.tensor_copy(pm, T.t16[:, 0:1]))
+    v(V.tensor_scalar(pm3, T.t16[:, 0:1], float(B), None, A.mult))
+    v(V.tensor_scalar(T.m16[:], T.t16[:], 0.0, 1.0 / SCALE, A.is_equal, A.mult))
+    v(V.memset(T.rmask[:, 0:H:16], -BIG))
+    V.wait_ge(sem.g1, 1)
+    V.tensor_copy(T.q0off[:], T.iI[:]).then_inc(sem.vq0, 1)
+    vw()
+    V.tensor_scalar(T.mE[:], T.iD[:], 0.0, even, A.is_equal, A.mult).then_inc(sem.vI, 1)
+    V.tensor_scalar(T.mO[:], T.iD[:], 0.0, odd, A.is_equal, A.mult).then_inc(sem.vI, 1)
+    V.wait_ge(sem.ldbr, 16)
+    v(V.tensor_copy(T.brF[:], T.brX[:]))
+    vw()
+    V.transpose(T.brT[:], T.brF[:]).then_inc(sem.vX, 1)
+    V.wait_ge(sem.g3, 3)
+    v(V.tensor_scalar(T.boI[:], T.iB[:], 4, None, A.arith_shift_right))
+    V.tensor_scalar(T.s2off[:], T.iS[:], pm3, None, A.add).then_inc(sem.vC, 1)
+    v(V.tensor_scalar(T.jj[:], T.iJ[:], pm, None, A.add))
+    vw()
+    M = H - 1
+    for s in range(N):
+        v(V.tensor_scalar(T.pX[:, s * H:(s + 1) * H], T.iI[:], float(pow(B, s, M)), None, A.mult))
+        v(V.tensor_scalar(T.pX[:, N * H + 4 * s:N * H + 4 * s + 4], T.jj[:, 0:4], float(pow(16, s + 1, M)), None, A.mult))
+    V.wait_ge(sem.pb, 1)
+    for h in range(2):
+        for U in range(8):
+            V.tensor_copy(T.brY[:, 2 * U + h:256:16], T.pB[:, 128 * h + 16 * U:128 * h + 16 * U + 16]).then_inc(sem.vY, 1)
+    vw()
+    v(V.tensor_scalar(T.pK[:], T.pX[:], 1.0 / M, -0.49, A.mult, A.add))
+    v(V.tensor_scalar(T.j47[:], T.jj[:], H - 1.0, H - 1.0, A.is_equal, A.mult))
+    vw()
+    v(V.tensor_copy(T.pKi[:], T.pK[:]))
+    V.tensor_scalar(T.bo[:], T.boI[:], 0.0, None, A.is_equal).then_inc(sem.vC, 1)
+    vw()
+    v(V.tensor_scalar(T.pK[:], T.pKi[:], -float(M), None, A.mult))
+    V.tensor_scalar(T.ebig[:, 15:143:16], T.boI[:, 0:128:16], 0.0, None, A.is_equal).then_inc(sem.vC, 1)
+    vw()
+    v(V.tensor_tensor(T.pR[:], T.pX[:], T.pK[:], A.add))
+    vw()
+    v(V.memset(T.pR[:, M:N * H:H], float(M)))
+    v(V.tensor_tensor(T.pR[:, N * H:], T.pR[:, N * H:], T.j47[:], A.add))
+    V.wait_ge(sem.lden, 16)
+    for w in range(2):
+        v(V.tensor_copy(T.lin[:, 8 * w:8 * w + B], T.ent[:, B * w:B * w + B]))
+    vw()
+    V.tensor_copy(T.poff[:], T.pR[:]).then_inc(sem.vq, 1)
+
+    def lst_in(n):
+        return T.lin[:, 8 * n:8 * n + B]
+
+    def lst_out(n):
+        return T.lout[:, 8 * n:8 * n + B]
+
+    def bridge_gather(c0, c1):
+        V.tensor_copy(T.nbbr[:, 16 * c0:16 * c1], T.nbI[:].indirect(T.brIn[:, c0:c1])).then_inc(sem.vnb, 1)
+
+    V.wait_ge(sem.ldnb, 16)
+    for w in range(2):
+        V.tensor_copy(wv(T.cf, w), T.nbI[:].indirect(lst_in(w))).then_inc(sm("vf", w), 1)
+        V.tensor_copy(wv(T.cu, w), T.nbI[:].indirect(lst_in(w))).then_inc(sm("v1", w), 1)
+    V.wait_ge(sem.arY, nin)
+    bridge_gather(0, PART1)
+    V.wait_ge(sem.ldk, 16)
+
+    def term_op(n):
+        s, w = divmod(n, 2)
+        V.wait_ge(sm("v7", w), s + 1)
+        V.wait_ge(sm("sc", w), s + 1)
+        V.tensor_tensor(wv(T.term, n), T.kS[:].indirect(lst_out(n)), wv(T.srep, n), A.mult).then_inc(sm("v8", w), 1)
+
+    for n in range(NW):
+        s, w = divmod(n, 2)
+        pU, pP = T["pU%d" % w], T["pP%d" % w]
+        if s >= 1:
+            if n == 2:
+                V.wait_ge(sem.vnb, 2)
+            V.wait_ge(sem["arl%d" % n], nin)
+            V.tensor_copy(wv(T.cu, n), T.nbbr[:].indirect(lst_in(n))).then_inc(sm("v1", w), 1)
+        V.wait_ge(sem["sq%d" % n], 1)
+        V.wait_ge(sm("v1", w), s + 1)
+        for (a0, a1), role in zip(CHUNKS, ("v2a", "v2b", "v2c")):
+            lo, hi = n * 16 * H + a0 * H, n * 16 * H + a1 * H
+            V.tensor_tensor(T.prod[:, lo:hi], T.kS[:].indirect(T.cu[:, n * H + B * a0:n * H + B * a1]), T.qrep[:, lo:hi],
+                            A.mult).then_inc(sm(role, w), 1)
+        V.wait_ge(sm("s2", w), s + 1)
+        V.transpose(T.dupT[:, B * n:B * n + B], T.dup[:, 2 * n * H:2 * (n + 1) * H]).then_inc(sm("vtr", w), 1)
+        if n >= 1:
+            term_op(n - 1)
+        V.wait_ge(sm("pu", w), s + 1)
+        V.tensor_tensor_scan(wv(T.rmax, n), T.rmask[:], pU[:, H - 1::-1], 0.0, A.add, A.max).then_inc(sm("v3", w), 1)
+        V.wait_ge(sm("v3", w), s + 1)
+        V.tensor_tensor(wv(T.dd, n), wv(T.rmax, n), pU[:, H - 1::-1], A.subtract).then_inc(sm("v4", w), 1)
+        V.wait_ge(sm("pp", w), s + 1)
+        V.wait_ge(sm("v4", w), s + 1)
+        V.tensor_tensor(wv(T.ee, n), pP[:, H - 1::-1], wv(T.dd, n), A.subtract).then_inc(sm("v5", w), 1)
+        V.wait_ge(sm("v5", w), s + 1)
+        V.tensor_tensor_scan(wv(T.sel, n), wv(T.dd, n), wv(T.ee, n), 0.0, A.min, A.max).then_inc(sm("v6", w), 1)
+        V.wait_ge(sm("v6", w), s + 1)
+        V.tensor_copy(lst_out(n), T.sel[:, n * H + H - 1:n * H:-16]).then_inc(sm("v7", w), 1)
+        if n == 1 and not SCALAR_BRIDGE:
+            bridge_gather(PART1, 256)
+    term_op(NW - 1)
+
+    PE.wait_ge(sem.vI, 2)
+    PE.wait_ge(sem.vX, 1)
+    keepE, upE, keepO, downO = T.mE[:, 16:144], T.mE[:, 0:128], T.mO[:, 16:144], T.mO[:, 32:160]
+    PE.matmul(T.pB[:, 0:128], keepE, T.brT[:, :, 0, :], True, False)
+    PE.matmul(T.pB[:, 0:128], upE, T.brT[:, :, 1, :], False, True)
+    PE.matmul(T.pB[:, 128:256], downO, T.brT[:, :, 0, :], True, False)
+    PE.matmul(T.pB[:, 128:256], keepO, T.brT[:, :, 1, :], False, True).then_inc(sem.pb, 1)
+    PE.wait_ge(sem.vC, 3)
+    for n in range(NW):
+        s, w = divmod(n, 2)
+        pU, pP, pS = T["pU%d" % w], T["pP%d" % w], T["pS%d" % w]
+        for (a0, a1), role in zip(CHUNKS, ("v2a", "v2b", "v2c")):
+            PE.wait_ge(sm(role, w), s + 1)
+            for a in range(a0, a1):
+                lo = n * 16 * H + a * H
+                mm = PE.matmul(pU[:, 0:H], T.ebig[:, 15 - a:143 - a], T.prod[:, lo:lo + H], a == 0, a == 15)
+        mm.then_inc(sm("pu", w), 1)
+        PE.wait_ge(sm("vtr", w), s + 1)
+        PE.matmul(pP[:, 0:H], keepE, T.dupT[:, B * n:B * n + B, 0, :], True, False)
+        PE.matmul(pP[:, 0:H], keepO, T.dupT[:, B * n:B * n + B, 1, :], False, True).then_inc(sm("pp", w), 1)
+        PE.wait_ge(sm("sr", w), B * (s + 1))
+        PE.matmul(pS[:, 0:H], T.bo[:], wv(T.rr, n), True, True).then_inc(sm("ps", w), 1)
+
+    seen = set()
+
+    def qrep(n):
+        s, w = divmod(n, 2)
+        if s >= 1 and s not in seen:
+            seen.add(s)
+            oc = cores[(rank - s) % N]
+            SC.wait_ge(sem["arq%d" % s], bits(topo.mask(oc if s == 1 else helper_of(oc, cores, topo), core)))
+        off = T.q0off[:] if s == 0 else T.poff[:, s * H:(s + 1) * H]
+        SC.activation(T.qrep[:, n * 16 * H:(n + 1) * 16 * H], wv(T.qall, n).indirect(off), F.Copy,
+                      scale=SCALE).then_inc(sem["sq%d" % n], 1)
+
+    def spread(n):
+        w = n % 2
+        SC.activation(T.dup[:, 2 * n * H:2 * (n + 1) * H], wv(T.cf, n).indirect(T.s2off[:, 0:2 * B]), F.Copy).then_inc(sm("s2", w), 1)
+
+    def unperm(n):
+        s, w = divmod(n, 2)
+        SC.wait_ge(sm("v8", w), s + 1)
+        if s >= 1:
+            SC.wait_ge(sm("su", w), s)
+        SC.activation(wv(T.termN, n), wv(T.term, n).indirect(T.poff[:, N * H + 4 * s:N * H + 4 * s + B]), F.Copy).then_inc(sm("su", w), 1)
+
+    SC.wait_ge(sem.vq0, 1)
+    SC.wait_ge(sem.ldq, 16)
+    qrep(0)
+    qrep(1)
+    SC.wait_ge(sem.vq, 1)
+    qrep(2)
+    SC.wait_ge(sem.vC, 3)
+    for w in range(2):
+        SC.wait_ge(sm("vf", w), 1)
+        spread(w)
+    if SCALAR_BRIDGE:
+        SC.wait_ge(sem.arY, nin)
+        SC.activation(T.nbbr[:, 16 * PART1:], T.nbI[:].indirect(T.brIn[:, PART1:256]), F.Copy).then_inc(sem.vnb, 1)
+    qrep(3)
+    ahead = 4 if SCALAR_BRIDGE else 5
+    for n in range(NW):
+        s, w = divmod(n, 2)
+        if s >= 1:
+            if n == 2:
+                SC.wait_ge(sem.vnb, 2)
+            SC.wait_ge(sem["arl%d" % n], nin)
+            SC.activation(wv(T.cf, n), T.nbbr[:].indirect(lst_in(n)), F.Copy).then_inc(sm("s1", w), 1)
+            SC.wait_ge(sm("s1", w), s)
+            spread(n)
+        if (s >= 1 or (SCALAR_BRIDGE and n == 1)) and n + ahead - (1 if SCALAR_BRIDGE else 0) < NW:
+            qrep(n + ahead - (1 if SCALAR_BRIDGE else 0))
+        if n >= 1:
+            unperm(n - 1)
+        SC.wait_ge(sm("v3", w), s + 1)
+        for b in range(B):
+            c = n * H + H - 1 - 16 * b
+            SC.activation(T.rr[:, n * H + 16 * b:n * H + 16 * b + 16], T.m16[:], F.Relu, scale=T.rmax[:, c:c + 1]).then_inc(sm("sr", w), 1)
+        SC.wait_ge(sm("ps", w), s + 1)
+        SC.activation(wv(T.srep, n), T["pS%d" % w][:, 0:H], F.Copy).then_inc(sm("sc", w), 1)
+        if n == 1 and not SCALAR_BRIDGE:
+            qrep(4)
+            qrep(5)
+            qrep(6)
+    unperm(NW - 1)

@@ -2,78 +2,47 @@ from concourse.bass import DstId, RemoteDMATransfer
 from concourse.mybir import AluOpType as A, ActivationFunctionType as F
 
 N, S, Q = 8, 4096, 96
-H = Q // 2
+W = 2
+H = Q // W
 B = H // 16
-NW = 2 * N
-CHUNKS = ((0, 8), (8, 14), (14, 16))
+NW = W * N
+NP = N * H + 32
+CHUNKS = (((0, 8), (8, 14), (14, 16)), ((0, 2), (2, 4), (4, 10), (10, 14), (14, 16)))
 PART1 = 128
-SCALAR_BRIDGE = True
 SCALE = 4096.0
 BIG = 1.0e9
 
+
+def _sb(n, d):
+    return ("sbuf", [128, n], d)
+
+
 SCRATCH = {
-    "nbI": ("sbuf", [128, S], "int32"),
-    "kS": ("sbuf", [128, S], "bfloat16"),
-    "nbbr": ("sbuf", [128, S], "float32"),
-    "qall": ("sbuf", [128, N * Q], "bfloat16"),
-    "qrep": ("sbuf", [128, NW * 16 * H], "bfloat16"),
-    "prod": ("sbuf", [128, NW * 16 * H], "bfloat16"),
-    "brX": ("sbuf", [128, 256], "int32"),
-    "brT": ("sbuf", [128, 8, 2, 16], "float32"),
-    "brY": ("sbuf", [128, 256], "uint16"),
-    "brIn": ("sbuf", [128, 256], "uint16"),
-    "ent": ("sbuf", [128, 8], "int32"),
-    "lin": ("sbuf", [128, NW * 8], "uint16"),
-    "lout": ("sbuf", [128, NW * 8], "uint16"),
-    "cu": ("sbuf", [128, NW * H], "uint16"),
-    "cf": ("sbuf", [128, NW * H], "float32"),
-    "dup": ("sbuf", [128, NW * 2 * H], "float32"),
-    "dupT": ("sbuf", [128, NW * B, 2, 16], "float32"),
-    "rmax": ("sbuf", [128, NW * H], "float32"),
-    "dd": ("sbuf", [128, NW * H], "float32"),
-    "ee": ("sbuf", [128, NW * H], "float32"),
-    "sel": ("sbuf", [128, NW * H], "float32"),
-    "rr": ("sbuf", [128, NW * H], "float32"),
-    "srep": ("sbuf", [128, NW * H], "float32"),
-    "term": ("sbuf", [128, NW * H], "float32"),
-    "termN": ("sbuf", [128, NW * H], "float32"),
-    "accin": ("sbuf", [128, (N + 1) * Q], "float32"),
-    "rmask": ("sbuf", [128, H], "float32"),
-    "ebig": ("sbuf", [128, 144], "bfloat16"),
-    "iI": ("sbuf", [128, H], "int32"),
-    "iP": ("sbuf", [128, 16], "int32"),
-    "iD": ("sbuf", [128, 160], "int32"),
-    "iB": ("sbuf", [128, 128], "int32"),
-    "iJ": ("sbuf", [128, 32], "int32"),
-    "iS": ("sbuf", [128, 8], "int32"),
-    "t16": ("sbuf", [128, 16], "int32"),
-    "evI": ("sbuf", [128, 4], "int32"),
-    "cols": ("sbuf", [128, 16], "float32"),
-    "m16": ("sbuf", [128, 16], "float32"),
-    "mE": ("sbuf", [128, 160], "float32"),
-    "mO": ("sbuf", [128, 160], "float32"),
-    "boI": ("sbuf", [128, 128], "int32"),
-    "bo": ("sbuf", [128, 128], "float32"),
-    "q0off": ("sbuf", [128, H], "uint16"),
-    "s2off": ("sbuf", [128, 8], "uint16"),
-    "jj": ("sbuf", [128, 32], "float32"),
-    "j47": ("sbuf", [128, 32], "float32"),
-    "brF": ("sbuf", [128, 256], "float32"),
-    "pX": ("sbuf", [128, 416], "float32"),
-    "pK": ("sbuf", [128, 416], "float32"),
-    "pKi": ("sbuf", [128, 416], "int32"),
-    "pR": ("sbuf", [128, 416], "float32"),
-    "poff": ("sbuf", [128, 416], "uint16"),
-    "pU0": ("psum", [128, 512], "float32"), "pU1": ("psum", [128, 512], "float32"),
-    "pP0": ("psum", [128, 512], "float32"), "pP1": ("psum", [128, 512], "float32"),
-    "pS0": ("psum", [128, 512], "float32"), "pS1": ("psum", [128, 512], "float32"),
-    "pB": ("psum", [128, 512], "float32"),
+    "nbI": _sb(S, "int32"), "kS": _sb(S, "bfloat16"), "nbbr": _sb(S, "float32"), "qall": _sb(N * Q, "bfloat16"),
+    "qrep": _sb(NW * 16 * H, "bfloat16"), "prod": _sb(NW * 16 * H, "bfloat16"),
+    "brX": _sb(256, "int32"), "brF": _sb(256, "float32"), "brT": ("sbuf", [128, 8, 2, 16], "float32"),
+    "brY": _sb(256, "uint16"), "brIn": _sb(256, "uint16"), "ent": _sb(8, "int32"),
+    "lin": _sb(NW * 8, "uint16"), "lout": _sb(NW * 8, "uint16"), "cu": _sb(NW * H, "uint16"),
+    "dup": _sb(NW * 2 * H, "float16"), "dupT": ("sbuf", [128, NW * B, 2, 16], "float16"),
+    "accin": _sb((N + 1) * Q, "float32"), "rmask": _sb(H, "float32"), "ebig": _sb(144, "bfloat16"),
+    "iI": _sb(H, "int32"), "iP": _sb(16, "int32"), "iD": _sb(160, "int32"), "iB": _sb(128, "int32"), "iJ": _sb(32, "int32"),
+    "iS": _sb(8, "int32"), "t16": _sb(16, "int32"), "evI": _sb(4, "int32"), "cols": _sb(20, "float32"), "m16": _sb(16, "float32"),
+    "mE": _sb(160, "float32"), "mO": _sb(160, "float32"), "hE": _sb(128, "float16"), "hO": _sb(128, "float16"),
+    "c16": _sb(128, "bfloat16"), "c1": _sb(H, "bfloat16"), "boI": _sb(128, "int32"), "bo": _sb(128, "float32"),
+    "q0off": _sb(H, "uint16"), "s2off": _sb(8, "uint16"), "jj": _sb(32, "float32"), "j47": _sb(32, "float32"),
+    "pX": _sb(NP, "float32"), "pK": _sb(NP, "float32"), "pKi": _sb(NP, "int32"), "pR": _sb(NP, "float32"),
+    "poff": _sb(NP, "uint16"),
 }
-ROLES = ["v1", "vf", "v2a", "v2b", "v2c", "vtr", "v3", "v4", "v5", "v6", "v7", "v8", "s1", "s2", "sr", "sc", "su", "pu", "pp", "ps"]
+for _n in ("cf", "rmax", "dd", "ee", "sel", "rr", "srep", "term", "termN"):
+    SCRATCH[_n] = _sb(NW * H, "float32")
+for _n in ("pU0", "pU1", "pP0", "pP1", "pS0", "pS1", "pB"):
+    SCRATCH[_n] = ("psum", [128, 512], "float32")
+ROLES = ["v1", "vf", "vtr", "v3", "v4", "v5", "v6", "v7", "v8", "s1", "s2", "sr", "sc", "su", "pu", "pp", "ps", "fin",
+         "v20", "v21", "v22", "v23", "v24"]
 SEMAPHORES = (["ldq", "ldbr", "lden", "ldnb", "ldk", "g1", "g2", "g3", "vs", "vq0", "vI", "vX", "vC", "vY", "vq", "vnb", "pb", "kgo",
-               "loc", "arY", "arH", "st", "fin0", "fin1"]
-              + ["%s_%d" % (r, w) for r in ROLES for w in range(2)]
-              + ["sq%d" % n for n in range(NW)] + ["arl%d" % n for n in range(2, NW)]
+               "loc", "arY", "arH", "st"]
+              + ["%s_%d" % (r, w) for r in ROLES for w in range(W)]
+              + ["sq%d" % n for n in range(NW)] + ["arl%d" % n for n in range(W, NW)]
               + ["ara%d" % s for s in range(1, N)] + ["arq%d" % s for s in range(1, N)])
 
 
@@ -159,8 +128,8 @@ def rank_program(g, core, T, topo):
     g.sem_inc(sem.kgo, 1)
 
     def send_acc(s):
-        g.wait_ge(sm("su", 0), s + 1)
-        g.wait_ge(sm("su", 1), s + 1)
+        for w in range(W):
+            g.wait_ge(sm("su", w), s + 1)
         dst = T.accin[:, (s + 1) * Q:(s + 2) * Q]
         src = T.termN[:, s * Q:(s + 1) * Q]
         if s == 0:
@@ -170,23 +139,23 @@ def rank_program(g, core, T, topo):
             send_sum(dst, [src, T.accin[:, s * Q:(s + 1) * Q]], sem["ara%d" % (s + 1)])
 
     for n in range(NW):
-        s, w = divmod(n, 2)
+        s, w = divmod(n, W)
         if s < N - 1:
             g.wait_ge(sm("v7", w), s + 1)
-            send(T.lin[:, 8 * (n + 2):8 * (n + 2) + 4], T.lout[:, 8 * n:8 * n + 4], sem["arl%d" % (n + 2)])
+            send(T.lin[:, 8 * (n + W):8 * (n + W) + 4], T.lout[:, 8 * n:8 * n + 4], sem["arl%d" % (n + W)])
         if w == 0 and s >= 1:
             send_acc(s - 1)
     g.wait_ge(sem["ara%d" % (N - 1)], nin)
-    for w in range(2):
-        n = NW - 2 + w
+    for w in range(W):
         g.wait_ge(sm("su", w), N)
-        send_sum(wv(T.accin, n + 2), [wv(T.termN, n), wv(T.accin, n)], sem["fin%d" % w])
+        n = NW - W + w
+        send_sum(wv(T.accin, n + W), [wv(T.termN, n), wv(T.accin, n)], sm("fin", w))
     g.wait_ge(sem.loc, loc[0])
 
-    for w in range(2):
-        SY.wait_ge(sem["fin%d" % w], nin)
+    for w in range(W):
+        SY.wait_ge(sm("fin", w), nin)
         SY.dma_start(T.y[:, w * H:(w + 1) * H], wv(T.accin, NW + w)).then_inc(sem.st, 16)
-    SY.wait_ge(sem.st, 32)
+    SY.wait_ge(sem.st, 16 * W)
 
     vs = [0]
 
@@ -197,10 +166,13 @@ def rank_program(g, core, T, topo):
     def vw():
         V.wait_ge(sem.vs, vs[0])
 
-    even, odd, pm, pm3 = T.cols[:, 0:1], T.cols[:, 4:5], T.cols[:, 8:9], T.cols[:, 12:13]
+    even, odd, pm, pm3, neg = (T.cols[:, 4 * i:4 * i + 1] for i in range(5))
     v(V.memset(T.rmask[:], 0.0))
     v(V.memset(T.ebig[:], 0.0))
     v(V.memset(T.lout[:], 0))
+    v(V.memset(T.c16[:], 16.0))
+    v(V.memset(T.c1[:], 1.0))
+    v(V.memset(neg, -2048.0))
     V.wait_ge(sem.g2, 2)
     v(V.tensor_scalar(T.t16[:], T.iP[:], 15, None, A.bitwise_and))
     v(V.tensor_scalar(T.evI[:, 0:1], T.iP[:, 0:1], 4, 1, A.arith_shift_right, A.bitwise_and))
@@ -228,14 +200,15 @@ def rank_program(g, core, T, topo):
     M = H - 1
     for s in range(N):
         v(V.tensor_scalar(T.pX[:, s * H:(s + 1) * H], T.iI[:], float(pow(B, s, M)), None, A.mult))
-        v(V.tensor_scalar(T.pX[:, N * H + 4 * s:N * H + 4 * s + 4], T.jj[:, 0:4], float(pow(16, s + 1, M)), None, A.mult))
     V.wait_ge(sem.pb, 1)
     for h in range(2):
         for U in range(8):
             V.tensor_copy(T.brY[:, 2 * U + h:256:16], T.pB[:, 128 * h + 16 * U:128 * h + 16 * U + 16]).then_inc(sem.vY, 1)
+    for s in range(N):
+        v(V.tensor_scalar(T.pX[:, N * H + 4 * s:N * H + 4 * s + 4], T.jj[:, 0:4], float(pow(16, s + 1, M)), None, A.mult))
     vw()
     v(V.tensor_scalar(T.pK[:], T.pX[:], 1.0 / M, -0.49, A.mult, A.add))
-    v(V.tensor_scalar(T.j47[:], T.jj[:], H - 1.0, H - 1.0, A.is_equal, A.mult))
+    v(V.tensor_scalar(T.j47[:], T.jj[:], float(M), float(M), A.is_equal, A.mult))
     vw()
     v(V.tensor_copy(T.pKi[:], T.pK[:]))
     V.tensor_scalar(T.bo[:], T.boI[:], 0.0, None, A.is_equal).then_inc(sem.vC, 1)
@@ -244,11 +217,13 @@ def rank_program(g, core, T, topo):
     V.tensor_scalar(T.ebig[:, 15:143:16], T.boI[:, 0:128:16], 0.0, None, A.is_equal).then_inc(sem.vC, 1)
     vw()
     v(V.tensor_tensor(T.pR[:], T.pX[:], T.pK[:], A.add))
+    V.tensor_scalar(T.hE[:], T.iD[:, 16:144], 0.0, even, A.is_equal, A.mult).then_inc(sem.vC, 1)
+    V.tensor_scalar(T.hO[:], T.iD[:, 16:144], 0.0, odd, A.is_equal, A.mult).then_inc(sem.vC, 1)
     vw()
     v(V.memset(T.pR[:, M:N * H:H], float(M)))
     v(V.tensor_tensor(T.pR[:, N * H:], T.pR[:, N * H:], T.j47[:], A.add))
     V.wait_ge(sem.lden, 16)
-    for w in range(2):
+    for w in range(W):
         v(V.tensor_copy(T.lin[:, 8 * w:8 * w + B], T.ent[:, B * w:B * w + B]))
     vw()
     V.tensor_copy(T.poff[:], T.pR[:]).then_inc(sem.vq, 1)
@@ -259,83 +234,94 @@ def rank_program(g, core, T, topo):
     def lst_out(n):
         return T.lout[:, 8 * n:8 * n + B]
 
-    def bridge_gather(c0, c1):
-        V.tensor_copy(T.nbbr[:, 16 * c0:16 * c1], T.nbI[:].indirect(T.brIn[:, c0:c1])).then_inc(sem.vnb, 1)
-
     V.wait_ge(sem.ldnb, 16)
-    for w in range(2):
+    for w in range(W):
         V.tensor_copy(wv(T.cf, w), T.nbI[:].indirect(lst_in(w))).then_inc(sm("vf", w), 1)
         V.tensor_copy(wv(T.cu, w), T.nbI[:].indirect(lst_in(w))).then_inc(sm("v1", w), 1)
     V.wait_ge(sem.arY, nin)
-    bridge_gather(0, PART1)
+    V.tensor_copy(T.nbbr[:, 0:16 * PART1], T.nbI[:].indirect(T.brIn[:, 0:PART1])).then_inc(sem.vnb, 1)
     V.wait_ge(sem.ldk, 16)
 
     def term_op(n):
-        s, w = divmod(n, 2)
+        s, w = divmod(n, W)
         V.wait_ge(sm("v7", w), s + 1)
         V.wait_ge(sm("sc", w), s + 1)
         V.tensor_tensor(wv(T.term, n), T.kS[:].indirect(lst_out(n)), wv(T.srep, n), A.mult).then_inc(sm("v8", w), 1)
 
-    for n in range(NW):
-        s, w = divmod(n, 2)
-        pU, pP = T["pU%d" % w], T["pP%d" % w]
-        if s >= 1:
-            if n == 2:
+    def neighbours(n):
+        if n >= W:
+            if n == W:
                 V.wait_ge(sem.vnb, 2)
             V.wait_ge(sem["arl%d" % n], nin)
-            V.tensor_copy(wv(T.cu, n), T.nbbr[:].indirect(lst_in(n))).then_inc(sm("v1", w), 1)
-        V.wait_ge(sem["sq%d" % n], 1)
-        V.wait_ge(sm("v1", w), s + 1)
-        for (a0, a1), role in zip(CHUNKS, ("v2a", "v2b", "v2c")):
-            lo, hi = n * 16 * H + a0 * H, n * 16 * H + a1 * H
-            V.tensor_tensor(T.prod[:, lo:hi], T.kS[:].indirect(T.cu[:, n * H + B * a0:n * H + B * a1]), T.qrep[:, lo:hi],
-                            A.mult).then_inc(sm(role, w), 1)
+            V.tensor_copy(wv(T.cu, n), T.nbbr[:].indirect(lst_in(n))).then_inc(sm("v1", n % W), 1)
+
+    def keys(n, i):
+        s, w = divmod(n, W)
+        if i == 0:
+            V.wait_ge(sem["sq%d" % n], 1)
+            V.wait_ge(sm("v1", w), s + 1)
+        a0, a1 = CHUNKS[w][i]
+        lo, hi = n * 16 * H + a0 * H, n * 16 * H + a1 * H
+        V.tensor_tensor(T.prod[:, lo:hi], T.kS[:].indirect(T.cu[:, n * H + B * a0:n * H + B * a1]), T.qrep[:, lo:hi],
+                        A.mult).then_inc(sm("v2%d" % i, w), 1)
+
+    for n in range(NW):
+        s, w = divmod(n, W)
+        pU, pP = T["pU%d" % w], T["pP%d" % w]
+        if w == 0:
+            neighbours(n)
+        for i in range(0 if w == 0 else 2, len(CHUNKS[w])):
+            keys(n, i)
         V.wait_ge(sm("s2", w), s + 1)
         V.transpose(T.dupT[:, B * n:B * n + B], T.dup[:, 2 * n * H:2 * (n + 1) * H]).then_inc(sm("vtr", w), 1)
         if n >= 1:
             term_op(n - 1)
         V.wait_ge(sm("pu", w), s + 1)
         V.tensor_tensor_scan(wv(T.rmax, n), T.rmask[:], pU[:, H - 1::-1], 0.0, A.add, A.max).then_inc(sm("v3", w), 1)
+        if w == 0:
+            neighbours(n + 1)
         V.wait_ge(sm("v3", w), s + 1)
         V.tensor_tensor(wv(T.dd, n), wv(T.rmax, n), pU[:, H - 1::-1], A.subtract).then_inc(sm("v4", w), 1)
         V.wait_ge(sm("pp", w), s + 1)
         V.wait_ge(sm("v4", w), s + 1)
         V.tensor_tensor(wv(T.ee, n), pP[:, H - 1::-1], wv(T.dd, n), A.subtract).then_inc(sm("v5", w), 1)
+        if w == 0:
+            keys(n + 1, 0)
         V.wait_ge(sm("v5", w), s + 1)
         V.tensor_tensor_scan(wv(T.sel, n), wv(T.dd, n), wv(T.ee, n), 0.0, A.min, A.max).then_inc(sm("v6", w), 1)
+        if w == 0:
+            keys(n + 1, 1)
         V.wait_ge(sm("v6", w), s + 1)
         V.tensor_copy(lst_out(n), T.sel[:, n * H + H - 1:n * H:-16]).then_inc(sm("v7", w), 1)
-        if n == 1 and not SCALAR_BRIDGE:
-            bridge_gather(PART1, 256)
     term_op(NW - 1)
 
     PE.wait_ge(sem.vI, 2)
     PE.wait_ge(sem.vX, 1)
-    keepE, upE, keepO, downO = T.mE[:, 16:144], T.mE[:, 0:128], T.mO[:, 16:144], T.mO[:, 32:160]
-    PE.matmul(T.pB[:, 0:128], keepE, T.brT[:, :, 0, :], True, False)
-    PE.matmul(T.pB[:, 0:128], upE, T.brT[:, :, 1, :], False, True)
-    PE.matmul(T.pB[:, 128:256], downO, T.brT[:, :, 0, :], True, False)
-    PE.matmul(T.pB[:, 128:256], keepO, T.brT[:, :, 1, :], False, True).then_inc(sem.pb, 1)
-    PE.wait_ge(sem.vC, 3)
+    PE.matmul(T.pB[:, 0:128], T.mE[:, 16:144], T.brT[:, :, 0, :], True, False)
+    PE.matmul(T.pB[:, 0:128], T.mE[:, 0:128], T.brT[:, :, 1, :], False, True)
+    PE.matmul(T.pB[:, 128:256], T.mO[:, 32:160], T.brT[:, :, 0, :], True, False)
+    PE.matmul(T.pB[:, 128:256], T.mO[:, 16:144], T.brT[:, :, 1, :], False, True).then_inc(sem.pb, 1)
+    PE.wait_ge(sem.vC, 5)
     for n in range(NW):
-        s, w = divmod(n, 2)
+        s, w = divmod(n, W)
         pU, pP, pS = T["pU%d" % w], T["pP%d" % w], T["pS%d" % w]
-        for (a0, a1), role in zip(CHUNKS, ("v2a", "v2b", "v2c")):
-            PE.wait_ge(sm(role, w), s + 1)
+        PE.matmul(pP[:, 0:H], T.c16[:], T.c1[:], True, False)
+        for i, (a0, a1) in enumerate(CHUNKS[w]):
+            PE.wait_ge(sm("v2%d" % i, w), s + 1)
             for a in range(a0, a1):
                 lo = n * 16 * H + a * H
                 mm = PE.matmul(pU[:, 0:H], T.ebig[:, 15 - a:143 - a], T.prod[:, lo:lo + H], a == 0, a == 15)
         mm.then_inc(sm("pu", w), 1)
         PE.wait_ge(sm("vtr", w), s + 1)
-        PE.matmul(pP[:, 0:H], keepE, T.dupT[:, B * n:B * n + B, 0, :], True, False)
-        PE.matmul(pP[:, 0:H], keepO, T.dupT[:, B * n:B * n + B, 1, :], False, True).then_inc(sm("pp", w), 1)
+        PE.matmul(pP[:, 0:H], T.hE[:], T.dupT[:, B * n:B * n + B, 0, :], False, False)
+        PE.matmul(pP[:, 0:H], T.hO[:], T.dupT[:, B * n:B * n + B, 1, :], False, True).then_inc(sm("pp", w), 1)
         PE.wait_ge(sm("sr", w), B * (s + 1))
         PE.matmul(pS[:, 0:H], T.bo[:], wv(T.rr, n), True, True).then_inc(sm("ps", w), 1)
 
     seen = set()
 
     def qrep(n):
-        s, w = divmod(n, 2)
+        s, w = divmod(n, W)
         if s >= 1 and s not in seen:
             seen.add(s)
             oc = cores[(rank - s) % N]
@@ -345,52 +331,54 @@ def rank_program(g, core, T, topo):
                       scale=SCALE).then_inc(sem["sq%d" % n], 1)
 
     def spread(n):
-        w = n % 2
-        SC.activation(T.dup[:, 2 * n * H:2 * (n + 1) * H], wv(T.cf, n).indirect(T.s2off[:, 0:2 * B]), F.Copy).then_inc(sm("s2", w), 1)
+        w = n % W
+        SC.activation(T.dup[:, 2 * n * H:2 * (n + 1) * H], wv(T.cf, n).indirect(T.s2off[:, 0:2 * B]), F.Identity,
+                      bias=neg).then_inc(sm("s2", w), 1)
 
     def unperm(n):
-        s, w = divmod(n, 2)
+        s, w = divmod(n, W)
         SC.wait_ge(sm("v8", w), s + 1)
         if s >= 1:
             SC.wait_ge(sm("su", w), s)
         SC.activation(wv(T.termN, n), wv(T.term, n).indirect(T.poff[:, N * H + 4 * s:N * H + 4 * s + B]), F.Copy).then_inc(sm("su", w), 1)
 
+    def score_copy(n):
+        s, w = divmod(n, W)
+        SC.wait_ge(sm("ps", w), s + 1)
+        SC.activation(wv(T.srep, n), T["pS%d" % w][:, 0:H], F.Copy).then_inc(sm("sc", w), 1)
+
     SC.wait_ge(sem.vq0, 1)
     SC.wait_ge(sem.ldq, 16)
-    qrep(0)
-    qrep(1)
+    for n in range(W):
+        qrep(n)
     SC.wait_ge(sem.vq, 1)
-    qrep(2)
-    SC.wait_ge(sem.vC, 3)
-    for w in range(2):
+    qrep(W)
+    SC.wait_ge(sem.vC, 5)
+    for w in range(W):
         SC.wait_ge(sm("vf", w), 1)
         spread(w)
-    if SCALAR_BRIDGE:
-        SC.wait_ge(sem.arY, nin)
-        SC.activation(T.nbbr[:, 16 * PART1:], T.nbI[:].indirect(T.brIn[:, PART1:256]), F.Copy).then_inc(sem.vnb, 1)
-    qrep(3)
-    ahead = 4 if SCALAR_BRIDGE else 5
+    SC.wait_ge(sem.arY, nin)
+    SC.activation(T.nbbr[:, 16 * PART1:], T.nbI[:].indirect(T.brIn[:, PART1:256]), F.Copy).then_inc(sem.vnb, 1)
+    qrep(W + 1)
     for n in range(NW):
-        s, w = divmod(n, 2)
+        s, w = divmod(n, W)
         if s >= 1:
-            if n == 2:
+            if n == W:
                 SC.wait_ge(sem.vnb, 2)
             SC.wait_ge(sem["arl%d" % n], nin)
             SC.activation(wv(T.cf, n), T.nbbr[:].indirect(lst_in(n)), F.Copy).then_inc(sm("s1", w), 1)
+        if n >= 1:
+            score_copy(n - 1)
+        if s >= 1:
             SC.wait_ge(sm("s1", w), s)
             spread(n)
-        if (s >= 1 or (SCALAR_BRIDGE and n == 1)) and n + ahead - (1 if SCALAR_BRIDGE else 0) < NW:
-            qrep(n + ahead - (1 if SCALAR_BRIDGE else 0))
-        if n >= 1:
-            unperm(n - 1)
+        if n >= 1 and n + W + 1 < NW:
+            qrep(n + W + 1)
         SC.wait_ge(sm("v3", w), s + 1)
         for b in range(B):
             c = n * H + H - 1 - 16 * b
             SC.activation(T.rr[:, n * H + 16 * b:n * H + 16 * b + 16], T.m16[:], F.Relu, scale=T.rmax[:, c:c + 1]).then_inc(sm("sr", w), 1)
-        SC.wait_ge(sm("ps", w), s + 1)
-        SC.activation(wv(T.srep, n), T["pS%d" % w][:, 0:H], F.Copy).then_inc(sm("sc", w), 1)
-        if n == 1 and not SCALAR_BRIDGE:
-            qrep(4)
-            qrep(5)
-            qrep(6)
+        if n >= 1:
+            unperm(n - 1)
+    score_copy(NW - 1)
     unperm(NW - 1)

@@ -5,11 +5,13 @@ N, S, Q = 8, 4096, 96
 W = 2
 H = Q // W
 B = H // 16
+M = H - 1
 NW = W * N
-NP = N * H + 32
 CHUNKS = (((0, 8), (8, 14), (14, 16)), ((0, 2), (2, 4), (4, 10), (10, 14), (14, 16)))
-PART1 = 128
-SCALE = 4096.0
+VECTOR = ("N0 K0 K0 K0 X0 T-1 A0 N1 B0 K1 C0 K1 D0", "K0 K0 K0 X0 T-1 A0 B0 C0 D0")
+TENSOR = ("U0 Z0 U0 U0 P0 S0", "U0 Z0 U0 U0 U0 U0 P0 S0")
+SCALAR = ("F0 Y-1 R0 Q2 L0 U-1",)
+PART1 = 112
 BIG = 1.0e9
 
 
@@ -20,26 +22,26 @@ def _sb(n, d):
 SCRATCH = {
     "nbI": _sb(S, "int32"), "kS": _sb(S, "bfloat16"), "nbbr": _sb(S, "float32"), "qall": _sb(N * Q, "bfloat16"),
     "qrep": _sb(NW * 16 * H, "bfloat16"), "prod": _sb(NW * 16 * H, "bfloat16"),
-    "brX": _sb(256, "int32"), "brF": _sb(256, "float32"), "brT": ("sbuf", [128, 8, 2, 16], "float32"),
-    "brY": _sb(256, "uint16"), "brIn": _sb(256, "uint16"), "ent": _sb(8, "int32"),
-    "lin": _sb(NW * 8, "uint16"), "lout": _sb(NW * 8, "uint16"), "cu": _sb(NW * H, "uint16"),
+    "brX": _sb(256, "int32"), "brF": _sb(256, "float16"), "brT": ("sbuf", [128, 8, 2, 16], "float16"),
+    "brY": ("sbuf", [128, 16, 16], "uint16"), "brIn": _sb(256, "uint16"), "ent": _sb(8, "int32"),
+    "lin": _sb(NW * 8, "uint16"), "lout": _sb(NW * 8, "uint16"), "cu": _sb(NW * H, "uint16"), "c0": _sb(Q, "float32"),
     "dup": _sb(NW * 2 * H, "float16"), "dupT": ("sbuf", [128, NW * B, 2, 16], "float16"),
     "accin": _sb((N + 1) * Q, "float32"), "rmask": _sb(H, "float32"), "ebig": _sb(144, "bfloat16"),
-    "iI": _sb(H, "int32"), "iP": _sb(16, "int32"), "iD": _sb(160, "int32"), "iB": _sb(128, "int32"), "iJ": _sb(32, "int32"),
-    "iS": _sb(8, "int32"), "t16": _sb(16, "int32"), "evI": _sb(4, "int32"), "cols": _sb(20, "float32"), "m16": _sb(16, "float32"),
-    "mE": _sb(160, "float32"), "mO": _sb(160, "float32"), "hE": _sb(128, "float16"), "hO": _sb(128, "float16"),
-    "c16": _sb(128, "bfloat16"), "c1": _sb(H, "bfloat16"), "boI": _sb(128, "int32"), "bo": _sb(128, "float32"),
-    "q0off": _sb(H, "uint16"), "s2off": _sb(8, "uint16"), "jj": _sb(32, "float32"), "j47": _sb(32, "float32"),
-    "pX": _sb(NP, "float32"), "pK": _sb(NP, "float32"), "pKi": _sb(NP, "int32"), "pR": _sb(NP, "float32"),
-    "poff": _sb(NP, "uint16"),
+    "iI": _sb(H, "int32"), "iP": _sb(16, "int32"), "iD": _sb(160, "int32"), "iB": _sb(128, "int32"), "iJ": _sb(64, "int32"),
+    "iS": _sb(8, "int32"), "t16": _sb(16, "int32"), "evI": _sb(4, "int32"), "cols": _sb(32, "float32"), "m16": _sb(16, "float32"),
+    "mE": _sb(160, "float16"), "mO": _sb(160, "float16"), "gE": _sb(128, "float16"), "gO": _sb(128, "float16"),
+    "c16": _sb(128, "bfloat16"), "c1": _sb(64, "bfloat16"), "boI": _sb(128, "int32"), "bo": _sb(128, "float16"),
+    "s2off": _sb(8, "uint16"), "jj": _sb(16, "float32"), "jM": _sb(64, "float32"),
+    "pX": _sb(64, "float32"), "pK": _sb(64, "float32"), "pKi": _sb(64, "int32"), "pR": _sb(64, "float32"),
+    "plst": _sb(64, "uint16"), "poff": _sb(64 * N, "uint16"), "rr": _sb(NW * H, "float16"),
 }
-for _n in ("cf", "rmax", "dd", "ee", "sel", "rr", "srep", "term", "termN"):
+for _n in ("cf", "rmax", "keep", "sel", "srep", "term", "termN"):
     SCRATCH[_n] = _sb(NW * H, "float32")
 for _n in ("pU0", "pU1", "pP0", "pP1", "pS0", "pS1", "pB"):
     SCRATCH[_n] = ("psum", [128, 512], "float32")
-ROLES = ["v1", "vf", "vtr", "v3", "v4", "v5", "v6", "v7", "v8", "s1", "s2", "sr", "sc", "su", "pu", "pp", "ps", "fin",
+ROLES = ["v1", "vf", "vtr", "v3", "v4", "v6", "v7", "v8", "s1", "s2", "sr", "sc", "su", "pu", "pp", "ps", "fin",
          "v20", "v21", "v22", "v23", "v24"]
-SEMAPHORES = (["ldq", "ldbr", "lden", "ldnb", "ldk", "g1", "g2", "g3", "vs", "vq0", "vI", "vX", "vC", "vY", "vq", "vnb", "pb", "kgo",
+SEMAPHORES = (["ldq", "ldbr", "lden", "ldnb", "ldk", "g1", "g2", "g3", "vs", "vI", "vX", "vC", "vY", "vq", "vnb", "pb", "kgo",
                "loc", "arY", "arH", "st"]
               + ["%s_%d" % (r, w) for r in ROLES for w in range(W)]
               + ["sq%d" % n for n in range(NW)] + ["arl%d" % n for n in range(W, NW)]
@@ -58,11 +60,9 @@ def bits(m):
 
 def helper_program(g, core, owner, T, topo):
     sem = T.sem
-    oc = T.cores[owner]
-    nxt = T.cores[(owner + 1) % N]
-    g.wait_ge(sem["arH"], bits(topo.mask(oc, core) & topo.mask(oc, nxt)))
+    g.wait_ge(sem["arH"], bits(topo.mask(T.cores[owner], core)))
     total = 0
-    for s in range(2, N):
+    for s in range(1, N):
         d = T.cores[(owner + s) % N]
         rid, pid, _ = topo.addr(d)
         m = topo.mask(core, d)
@@ -94,6 +94,9 @@ def rank_program(g, core, T, topo):
     def wv(buf, n):
         return buf[:, n * H:(n + 1) * H]
 
+    def plist(e):
+        return T.plst[:, 4 * (e + N - 1):4 * (e + N - 1) + B]
+
     SY.dma_start(T.brX[:], T.br[:]).then_inc(sem.ldbr, 16)
     SC.dma_start(T.qall[:, 0:Q], T.q[:]).then_inc(sem.ldq, 16)
     SC.dma_start(T.ent[:, 0:6], T.entry[:]).then_inc(sem.lden, 16)
@@ -104,8 +107,8 @@ def rank_program(g, core, T, topo):
     g.iota(T.iP[:], [[-1, 16]], 16, 1).then_inc(sem.g2, 1)
     g.iota(T.iD[:], [[-1, 160]], 16, 1).then_inc(sem.g2, 1)
     g.iota(T.iI[:], [[1, H]], 0, 0).then_inc(sem.g1, 1)
+    g.iota(T.iJ[:], [[0, 16], [16, 4]], 0, 0).then_inc(sem.g1, 1)
     g.iota(T.iB[:], [[-16, 8], [0, 16]], 0, 1).then_inc(sem.g3, 1)
-    g.iota(T.iJ[:], [[0, 8], [16, 4]], 0, 0).then_inc(sem.g3, 1)
     g.iota(T.iS[:], [[1, 4], [0, 2]], 0, 0).then_inc(sem.g3, 1)
 
     def send(dst, src, rsem):
@@ -118,12 +121,11 @@ def rank_program(g, core, T, topo):
         loc[0] += bits(nmask)
 
     g.wait_ge(sem.ldq, 16)
-    send(T.qall[:, Q:2 * Q], T.qall[:, 0:Q], sem.arq1)
     hrid, hpid, _ = topo.addr(hlp)
-    hmask = topo.mask(core, hlp) & nmask
+    hmask = topo.mask(core, hlp)
     g.remote_dma(T.qall[:, 0:Q], T.qall[:, 0:Q], sem.arH, sem.loc, hpid, hrid, hmask)
     loc[0] += bits(hmask)
-    g.wait_ge(sem.vY, 16)
+    g.wait_ge(sem.vY, 8)
     send(T.brIn[:], T.brY[:], sem.arY)
     g.sem_inc(sem.kgo, 1)
 
@@ -147,9 +149,9 @@ def rank_program(g, core, T, topo):
             send_acc(s - 1)
     g.wait_ge(sem["ara%d" % (N - 1)], nin)
     for w in range(W):
-        g.wait_ge(sm("su", w), N)
+        g.wait_ge(sm("v8", w), N)
         n = NW - W + w
-        send_sum(wv(T.accin, n + W), [wv(T.termN, n), wv(T.accin, n)], sm("fin", w))
+        send_sum(wv(T.accin, n + W), [wv(T.term, n), wv(T.accin, n)], sm("fin", w))
     g.wait_ge(sem.loc, loc[0])
 
     for w in range(W):
@@ -166,12 +168,12 @@ def rank_program(g, core, T, topo):
     def vw():
         V.wait_ge(sem.vs, vs[0])
 
-    even, odd, pm, pm3, neg = (T.cols[:, 4 * i:4 * i + 1] for i in range(5))
+    even, odd, pm, pm3, neg, neven, nodd, pmM = (T.cols[:, 4 * i:4 * i + 1] for i in range(8))
     v(V.memset(T.rmask[:], 0.0))
     v(V.memset(T.ebig[:], 0.0))
     v(V.memset(T.lout[:], 0))
     v(V.memset(T.c16[:], 16.0))
-    v(V.memset(T.c1[:], 1.0))
+    v(V.memset(T.c1[:], 0.0))
     v(V.memset(neg, -2048.0))
     V.wait_ge(sem.g2, 2)
     v(V.tensor_scalar(T.t16[:], T.iP[:], 15, None, A.bitwise_and))
@@ -181,52 +183,51 @@ def rank_program(g, core, T, topo):
     v(V.tensor_scalar(odd, T.evI[:, 0:1], -1.0, 1.0, A.mult, A.add))
     v(V.tensor_copy(pm, T.t16[:, 0:1]))
     v(V.tensor_scalar(pm3, T.t16[:, 0:1], float(B), None, A.mult))
-    v(V.tensor_scalar(T.m16[:], T.t16[:], 0.0, 1.0 / SCALE, A.is_equal, A.mult))
+    v(V.tensor_scalar(T.m16[:], T.t16[:], 0.0, None, A.is_equal))
     v(V.memset(T.rmask[:, 0:H:16], -BIG))
-    V.wait_ge(sem.g1, 1)
-    V.tensor_copy(T.q0off[:], T.iI[:]).then_inc(sem.vq0, 1)
+    v(V.memset(T.c1[:, 0:H:16], 1.0))
+    v(V.tensor_scalar(neven, T.evI[:, 0:1], -1.0, None, A.mult))
+    v(V.tensor_scalar(nodd, T.evI[:, 0:1], 1.0, None, A.subtract))
+    v(V.tensor_scalar(pmM, T.t16[:, 0:1], -1.0, float(M), A.mult, A.add))
     vw()
     V.tensor_scalar(T.mE[:], T.iD[:], 0.0, even, A.is_equal, A.mult).then_inc(sem.vI, 1)
     V.tensor_scalar(T.mO[:], T.iD[:], 0.0, odd, A.is_equal, A.mult).then_inc(sem.vI, 1)
+    V.wait_ge(sem.g1, 2)
+    for r in range(4):
+        v(V.tensor_scalar(T.jj[:, 4 * r:4 * r + 4], T.iJ[:, 0:4], pm, float(pow(16, r, M)), A.add, A.mult))
+    v(V.tensor_scalar(T.jM[:], T.iJ[:], pmM, float(M), A.is_equal, A.mult))
+    vw()
+    for r in range(4):
+        v(V.tensor_scalar(T.pX[:, 16 * r:16 * r + 16], T.jj[:], float(pow(16, 4 * r + 1 - N, M)), None, A.mult))
     V.wait_ge(sem.ldbr, 16)
-    v(V.tensor_copy(T.brF[:], T.brX[:]))
+    v(V.tensor_scalar(T.brF[:], T.brX[:], -2048.0, None, A.add))
     vw()
     V.transpose(T.brT[:], T.brF[:]).then_inc(sem.vX, 1)
-    V.wait_ge(sem.g3, 3)
-    v(V.tensor_scalar(T.boI[:], T.iB[:], 4, None, A.arith_shift_right))
-    V.tensor_scalar(T.s2off[:], T.iS[:], pm3, None, A.add).then_inc(sem.vC, 1)
-    v(V.tensor_scalar(T.jj[:], T.iJ[:], pm, None, A.add))
-    vw()
-    M = H - 1
-    for s in range(N):
-        v(V.tensor_scalar(T.pX[:, s * H:(s + 1) * H], T.iI[:], float(pow(B, s, M)), None, A.mult))
-    V.wait_ge(sem.pb, 1)
-    for h in range(2):
-        for U in range(8):
-            V.tensor_copy(T.brY[:, 2 * U + h:256:16], T.pB[:, 128 * h + 16 * U:128 * h + 16 * U + 16]).then_inc(sem.vY, 1)
-    for s in range(N):
-        v(V.tensor_scalar(T.pX[:, N * H + 4 * s:N * H + 4 * s + 4], T.jj[:, 0:4], float(pow(16, s + 1, M)), None, A.mult))
-    vw()
     v(V.tensor_scalar(T.pK[:], T.pX[:], 1.0 / M, -0.49, A.mult, A.add))
-    v(V.tensor_scalar(T.j47[:], T.jj[:], float(M), float(M), A.is_equal, A.mult))
+    v(V.tensor_tensor(T.pR[:], T.pX[:], T.jM[:], A.add))
+    V.wait_ge(sem.g3, 2)
+    v(V.tensor_scalar(T.boI[:], T.iB[:], 4, None, A.arith_shift_right))
     vw()
     v(V.tensor_copy(T.pKi[:], T.pK[:]))
-    V.tensor_scalar(T.bo[:], T.boI[:], 0.0, None, A.is_equal).then_inc(sem.vC, 1)
+    V.wait_ge(sem.pb, 1)
+    for U in range(8):
+        V.tensor_scalar(T.brY[:, :, 2 * U:2 * U + 2], T.pB[:, 32 * U:32 * U + 32], 2048.0, None, A.add).then_inc(sem.vY, 1)
     vw()
     v(V.tensor_scalar(T.pK[:], T.pKi[:], -float(M), None, A.mult))
+    V.tensor_scalar(T.s2off[:], T.iS[:], pm3, None, A.add).then_inc(sem.vC, 1)
+    V.tensor_scalar(T.bo[:], T.boI[:], 0.0, None, A.is_equal).then_inc(sem.vC, 1)
+    vw()
+    v(V.tensor_tensor(T.pX[:], T.pR[:], T.pK[:], A.add))
     V.tensor_scalar(T.ebig[:, 15:143:16], T.boI[:, 0:128:16], 0.0, None, A.is_equal).then_inc(sem.vC, 1)
+    V.tensor_scalar(T.gE[:], T.iD[:, 16:144], 0.0, neven, A.is_equal, A.mult).then_inc(sem.vC, 1)
     vw()
-    v(V.tensor_tensor(T.pR[:], T.pX[:], T.pK[:], A.add))
-    V.tensor_scalar(T.hE[:], T.iD[:, 16:144], 0.0, even, A.is_equal, A.mult).then_inc(sem.vC, 1)
-    V.tensor_scalar(T.hO[:], T.iD[:, 16:144], 0.0, odd, A.is_equal, A.mult).then_inc(sem.vC, 1)
-    vw()
-    v(V.memset(T.pR[:, M:N * H:H], float(M)))
-    v(V.tensor_tensor(T.pR[:, N * H:], T.pR[:, N * H:], T.j47[:], A.add))
+    v(V.tensor_copy(T.plst[:], T.pX[:]))
+    V.tensor_scalar(T.gO[:], T.iD[:, 16:144], 0.0, nodd, A.is_equal, A.mult).then_inc(sem.vC, 1)
     V.wait_ge(sem.lden, 16)
     for w in range(W):
         v(V.tensor_copy(T.lin[:, 8 * w:8 * w + B], T.ent[:, B * w:B * w + B]))
     vw()
-    V.tensor_copy(T.poff[:], T.pR[:]).then_inc(sem.vq, 1)
+    V.tensor_copy(T.poff[:], T.iI[:].indirect(T.plst[:, 4 * N:8 * N])).then_inc(sem.vq, 1)
 
     def lst_in(n):
         return T.lin[:, 8 * n:8 * n + B]
@@ -236,8 +237,11 @@ def rank_program(g, core, T, topo):
 
     V.wait_ge(sem.ldnb, 16)
     for w in range(W):
-        V.tensor_copy(wv(T.cf, w), T.nbI[:].indirect(lst_in(w))).then_inc(sm("vf", w), 1)
-        V.tensor_copy(wv(T.cu, w), T.nbI[:].indirect(lst_in(w))).then_inc(sm("v1", w), 1)
+        v(V.tensor_copy(wv(T.c0, w), T.nbI[:].indirect(lst_in(w))))
+    vw()
+    for w in range(W):
+        V.tensor_copy(wv(T.cf, w), wv(T.c0, w).indirect(plist(N))).then_inc(sm("vf", w), 1)
+        V.tensor_copy(wv(T.cu, w), wv(T.c0, w).indirect(plist(N))).then_inc(sm("v1", w), 1)
     V.wait_ge(sem.arY, nin)
     V.tensor_copy(T.nbbr[:, 0:16 * PART1], T.nbI[:].indirect(T.brIn[:, 0:PART1])).then_inc(sem.vnb, 1)
     V.wait_ge(sem.ldk, 16)
@@ -248,75 +252,89 @@ def rank_program(g, core, T, topo):
         V.wait_ge(sm("sc", w), s + 1)
         V.tensor_tensor(wv(T.term, n), T.kS[:].indirect(lst_out(n)), wv(T.srep, n), A.mult).then_inc(sm("v8", w), 1)
 
-    def neighbours(n):
-        if n >= W:
+    piece = [0] * NW
+
+    def vec(c, n):
+        s, w = divmod(n, W)
+        pU, pP = T["pU%d" % (n % 2)], T["pP%d" % (n % 2)]
+        if c == "N" and n >= W:
             if n == W:
                 V.wait_ge(sem.vnb, 2)
             V.wait_ge(sem["arl%d" % n], nin)
-            V.tensor_copy(wv(T.cu, n), T.nbbr[:].indirect(lst_in(n))).then_inc(sm("v1", n % W), 1)
+            V.tensor_copy(wv(T.cu, n), T.nbbr[:].indirect(lst_in(n))).then_inc(sm("v1", w), 1)
+        elif c == "K":
+            i = piece[n]
+            piece[n] += 1
+            if i == 0:
+                V.wait_ge(sem["sq%d" % n], 1)
+                V.wait_ge(sm("v1", w), s + 1)
+            a0, a1 = CHUNKS[w][i]
+            lo, hi = n * 16 * H + a0 * H, n * 16 * H + a1 * H
+            V.tensor_tensor(T.prod[:, lo:hi], T.kS[:].indirect(T.cu[:, n * H + B * a0:n * H + B * a1]), T.qrep[:, lo:hi],
+                            A.mult).then_inc(sm("v2%d" % i, w), 1)
+        elif c == "X":
+            V.wait_ge(sm("s2", w), s + 1)
+            V.transpose(T.dupT[:, B * n:B * n + B], T.dup[:, 2 * n * H:2 * (n + 1) * H]).then_inc(sm("vtr", w), 1)
+        elif c == "T":
+            term_op(n)
+        elif c == "A":
+            V.wait_ge(sm("pu", w), s + 1)
+            V.tensor_tensor_scan(wv(T.rmax, n), T.rmask[:], pU[:, H - 1::-1], 0.0, A.add, A.max).then_inc(sm("v3", w), 1)
+        elif c == "B":
+            V.wait_ge(sm("v3", w), s + 1)
+            V.tensor_tensor(wv(T.keep, n), wv(T.rmax, n), pU[:, H - 1::-1], A.is_gt).then_inc(sm("v4", w), 1)
+        elif c == "C":
+            V.wait_ge(sm("pp", w), s + 1)
+            V.wait_ge(sm("v4", w), s + 1)
+            V.tensor_tensor_scan(wv(T.sel, n), wv(T.keep, n), pP[:, H - 1::-1], 0.0, A.mult, A.add).then_inc(sm("v6", w), 1)
+        elif c == "D":
+            V.wait_ge(sm("v6", w), s + 1)
+            V.tensor_copy(lst_out(n), T.sel[:, n * H + H - 1:n * H:-16]).then_inc(sm("v7", w), 1)
 
-    def keys(n, i):
-        s, w = divmod(n, W)
-        if i == 0:
-            V.wait_ge(sem["sq%d" % n], 1)
-            V.wait_ge(sm("v1", w), s + 1)
-        a0, a1 = CHUNKS[w][i]
-        lo, hi = n * 16 * H + a0 * H, n * 16 * H + a1 * H
-        V.tensor_tensor(T.prod[:, lo:hi], T.kS[:].indirect(T.cu[:, n * H + B * a0:n * H + B * a1]), T.qrep[:, lo:hi],
-                        A.mult).then_inc(sm("v2%d" % i, w), 1)
+    def slots(order, call):
+        for m in range(-W, NW + W):
+            for tok in order[m % len(order)].split():
+                n = m + int(tok[1:])
+                if 0 <= n < NW:
+                    call(tok[0], n)
 
-    for n in range(NW):
-        s, w = divmod(n, W)
-        pU, pP = T["pU%d" % w], T["pP%d" % w]
-        if w == 0:
-            neighbours(n)
-        for i in range(0 if w == 0 else 2, len(CHUNKS[w])):
-            keys(n, i)
-        V.wait_ge(sm("s2", w), s + 1)
-        V.transpose(T.dupT[:, B * n:B * n + B], T.dup[:, 2 * n * H:2 * (n + 1) * H]).then_inc(sm("vtr", w), 1)
-        if n >= 1:
-            term_op(n - 1)
-        V.wait_ge(sm("pu", w), s + 1)
-        V.tensor_tensor_scan(wv(T.rmax, n), T.rmask[:], pU[:, H - 1::-1], 0.0, A.add, A.max).then_inc(sm("v3", w), 1)
-        if w == 0:
-            neighbours(n + 1)
-        V.wait_ge(sm("v3", w), s + 1)
-        V.tensor_tensor(wv(T.dd, n), wv(T.rmax, n), pU[:, H - 1::-1], A.subtract).then_inc(sm("v4", w), 1)
-        V.wait_ge(sm("pp", w), s + 1)
-        V.wait_ge(sm("v4", w), s + 1)
-        V.tensor_tensor(wv(T.ee, n), pP[:, H - 1::-1], wv(T.dd, n), A.subtract).then_inc(sm("v5", w), 1)
-        if w == 0:
-            keys(n + 1, 0)
-        V.wait_ge(sm("v5", w), s + 1)
-        V.tensor_tensor_scan(wv(T.sel, n), wv(T.dd, n), wv(T.ee, n), 0.0, A.min, A.max).then_inc(sm("v6", w), 1)
-        if w == 0:
-            keys(n + 1, 1)
-        V.wait_ge(sm("v6", w), s + 1)
-        V.tensor_copy(lst_out(n), T.sel[:, n * H + H - 1:n * H:-16]).then_inc(sm("v7", w), 1)
-    term_op(NW - 1)
+    slots(VECTOR, vec)
 
     PE.wait_ge(sem.vI, 2)
     PE.wait_ge(sem.vX, 1)
-    PE.matmul(T.pB[:, 0:128], T.mE[:, 16:144], T.brT[:, :, 0, :], True, False)
-    PE.matmul(T.pB[:, 0:128], T.mE[:, 0:128], T.brT[:, :, 1, :], False, True)
-    PE.matmul(T.pB[:, 128:256], T.mO[:, 32:160], T.brT[:, :, 0, :], True, False)
-    PE.matmul(T.pB[:, 128:256], T.mO[:, 16:144], T.brT[:, :, 1, :], False, True).then_inc(sem.pb, 1)
+    PE.matmul(T.pB[:, 0:256:2], T.mE[:, 16:144], T.brT[:, :, 0, :], True, False)
+    PE.matmul(T.pB[:, 0:256:2], T.mE[:, 0:128], T.brT[:, :, 1, :], False, True)
+    PE.matmul(T.pB[:, 1:256:2], T.mO[:, 32:160], T.brT[:, :, 0, :], True, False)
+    PE.matmul(T.pB[:, 1:256:2], T.mO[:, 16:144], T.brT[:, :, 1, :], False, True).then_inc(sem.pb, 1)
     PE.wait_ge(sem.vC, 5)
-    for n in range(NW):
+    done = [0] * NW
+
+    def ten(c, n):
         s, w = divmod(n, W)
-        pU, pP, pS = T["pU%d" % w], T["pP%d" % w], T["pS%d" % w]
-        PE.matmul(pP[:, 0:H], T.c16[:], T.c1[:], True, False)
-        for i, (a0, a1) in enumerate(CHUNKS[w]):
+        pU, pP, pS = T["pU%d" % (n % 2)], T["pP%d" % (n % 2)], T["pS%d" % (n % 2)]
+        if c == "U":
+            i = done[n]
+            done[n] += 1
             PE.wait_ge(sm("v2%d" % i, w), s + 1)
-            for a in range(a0, a1):
+            for a in range(*CHUNKS[w][i]):
                 lo = n * 16 * H + a * H
                 mm = PE.matmul(pU[:, 0:H], T.ebig[:, 15 - a:143 - a], T.prod[:, lo:lo + H], a == 0, a == 15)
-        mm.then_inc(sm("pu", w), 1)
-        PE.wait_ge(sm("vtr", w), s + 1)
-        PE.matmul(pP[:, 0:H], T.hE[:], T.dupT[:, B * n:B * n + B, 0, :], False, False)
-        PE.matmul(pP[:, 0:H], T.hO[:], T.dupT[:, B * n:B * n + B, 1, :], False, True).then_inc(sm("pp", w), 1)
-        PE.wait_ge(sm("sr", w), B * (s + 1))
-        PE.matmul(pS[:, 0:H], T.bo[:], wv(T.rr, n), True, True).then_inc(sm("ps", w), 1)
+            if a == 15:
+                mm.then_inc(sm("pu", w), 1)
+        elif c == "Z":
+            PE.matmul(pP[:, 0:H + 16], T.c16[:], T.c1[:, 0:H + 16], True, False)
+        elif c == "P":
+            PE.wait_ge(sm("vtr", w), s + 1)
+            for h, (plus, minus) in enumerate(((T.mE[:, 16:144], T.gE[:]), (T.mO[:, 16:144], T.gO[:]))):
+                PE.matmul(pP[:, 0:H], plus, T.dupT[:, B * n:B * n + B, h, :], False, False)
+                PE.matmul(pP[:, 1:H + 1], minus, T.dupT[:, B * n:B * n + B, h, :], False, False)
+                mm = PE.matmul(pP[:, 16:H + 1:16], plus, T.dupT[:, B * n:B * n + B, h, 15], False, h == 1)
+            mm.then_inc(sm("pp", w), 1)
+        else:
+            PE.wait_ge(sm("sr", w), B * (s + 1))
+            PE.matmul(pS[:, 0:H], T.bo[:], wv(T.rr, n), True, True).then_inc(sm("ps", w), 1)
+
+    slots(TENSOR, ten)
 
     seen = set()
 
@@ -324,11 +342,9 @@ def rank_program(g, core, T, topo):
         s, w = divmod(n, W)
         if s >= 1 and s not in seen:
             seen.add(s)
-            oc = cores[(rank - s) % N]
-            SC.wait_ge(sem["arq%d" % s], bits(topo.mask(oc if s == 1 else helper_of(oc, cores, topo), core)))
-        off = T.q0off[:] if s == 0 else T.poff[:, s * H:(s + 1) * H]
-        SC.activation(T.qrep[:, n * 16 * H:(n + 1) * 16 * H], wv(T.qall, n).indirect(off), F.Copy,
-                      scale=SCALE).then_inc(sem["sq%d" % n], 1)
+            SC.wait_ge(sem["arq%d" % s], bits(topo.mask(helper_of(cores[(rank - s) % N], cores, topo), core)))
+        SC.activation(T.qrep[:, n * 16 * H:(n + 1) * 16 * H], wv(T.qall, n).indirect(T.poff[:, 64 * (N - 1 - s):64 * (N - 1 - s) + H]),
+                      F.Copy).then_inc(sem["sq%d" % n], 1)
 
     def spread(n):
         w = n % W
@@ -337,48 +353,49 @@ def rank_program(g, core, T, topo):
 
     def unperm(n):
         s, w = divmod(n, W)
-        SC.wait_ge(sm("v8", w), s + 1)
-        if s >= 1:
-            SC.wait_ge(sm("su", w), s)
-        SC.activation(wv(T.termN, n), wv(T.term, n).indirect(T.poff[:, N * H + 4 * s:N * H + 4 * s + B]), F.Copy).then_inc(sm("su", w), 1)
+        if s < N - 1:
+            SC.wait_ge(sm("v8", w), s + 1)
+            if s >= 1:
+                SC.wait_ge(sm("su", w), s)
+            SC.activation(wv(T.termN, n), wv(T.term, n).indirect(plist(s + 1 - N)), F.Copy).then_inc(sm("su", w), 1)
 
     def score_copy(n):
         s, w = divmod(n, W)
         SC.wait_ge(sm("ps", w), s + 1)
-        SC.activation(wv(T.srep, n), T["pS%d" % w][:, 0:H], F.Copy).then_inc(sm("sc", w), 1)
+        SC.activation(wv(T.srep, n), T["pS%d" % (n % 2)][:, 0:H], F.Copy).then_inc(sm("sc", w), 1)
 
-    SC.wait_ge(sem.vq0, 1)
+    SC.wait_ge(sem.vq, 1)
     SC.wait_ge(sem.ldq, 16)
     for n in range(W):
         qrep(n)
-    SC.wait_ge(sem.vq, 1)
-    qrep(W)
     SC.wait_ge(sem.vC, 5)
     for w in range(W):
         SC.wait_ge(sm("vf", w), 1)
         spread(w)
     SC.wait_ge(sem.arY, nin)
     SC.activation(T.nbbr[:, 16 * PART1:], T.nbI[:].indirect(T.brIn[:, PART1:256]), F.Copy).then_inc(sem.vnb, 1)
-    qrep(W + 1)
-    for n in range(NW):
+
+    def sca(c, n):
         s, w = divmod(n, W)
-        if s >= 1:
+        if c == "F" and s >= 1:
             if n == W:
                 SC.wait_ge(sem.vnb, 2)
             SC.wait_ge(sem["arl%d" % n], nin)
             SC.activation(wv(T.cf, n), T.nbbr[:].indirect(lst_in(n)), F.Copy).then_inc(sm("s1", w), 1)
-        if n >= 1:
-            score_copy(n - 1)
-        if s >= 1:
+        elif c == "R" and s >= 1:
             SC.wait_ge(sm("s1", w), s)
             spread(n)
-        if n >= 1 and n + W + 1 < NW:
-            qrep(n + W + 1)
-        SC.wait_ge(sm("v3", w), s + 1)
-        for b in range(B):
-            c = n * H + H - 1 - 16 * b
-            SC.activation(T.rr[:, n * H + 16 * b:n * H + 16 * b + 16], T.m16[:], F.Relu, scale=T.rmax[:, c:c + 1]).then_inc(sm("sr", w), 1)
-        if n >= 1:
-            unperm(n - 1)
-    score_copy(NW - 1)
-    unperm(NW - 1)
+        elif c == "Q" and s >= 1:
+            qrep(n)
+        elif c == "L":
+            SC.wait_ge(sm("v3", w), s + 1)
+            for b in range(B):
+                c = n * H + H - 1 - 16 * b
+                SC.activation(T.rr[:, n * H + 16 * b:n * H + 16 * b + 16], T.m16[:], F.Relu,
+                              scale=T.rmax[:, c:c + 1]).then_inc(sm("sr", w), 1)
+        elif c == "Y":
+            score_copy(n)
+        elif c == "U":
+            unperm(n)
+
+    slots(SCALAR, sca)

@@ -2,17 +2,20 @@ from concourse.bass import DstId, RemoteDMATransfer
 from concourse.mybir import AluOpType as A, ActivationFunctionType as F
 
 N, S, Q = 8, 4096, 96
-W = 2
+W = 3
 H = Q // W
 B = H // 16
-M = H - 1
 NW = W * N
-CHUNKS = (((0, 8), (8, 14), (14, 16)), ((0, 2), (2, 4), (4, 10), (10, 14), (14, 16)))
-VECTOR = ("N0 K0 K0 K0 X0 T-1 A0 N1 B0 K1 C0 K1 D0", "K0 K0 K0 X0 T-1 A0 B0 C0 D0")
-TENSOR = ("U0 Z0 U0 U0 P0 S0", "U0 Z0 U0 U0 U0 U0 P0 S0")
-SCALAR = ("F0 Y-1 R0 Q2 L0 U-1",)
-PART1 = 112
+QS = Q + 16
+ZW = 64 * H + 16
+CHUNKS = ((0, 16), (16, 28), (28, 32))
+VECTOR = ("A0 T-1 B0 L0 C0 X1 Z2 Z2 Y0", "A0 T-1 B0 L0 C0 Y0 T0")
+TENSOR = ("P0 M1 U1 S0 U1 U1", "P0 S0")
+SCALAR = ("N1 F1 G1 G1 G1", "")
+PART1 = 144
+SUMS = 0
 BIG = 1.0e9
+OUT = 1048576.0
 
 
 def _sb(n, d):
@@ -20,32 +23,29 @@ def _sb(n, d):
 
 
 SCRATCH = {
-    "nbI": _sb(S, "int32"), "kS": _sb(S, "bfloat16"), "nbbr": _sb(S, "float32"), "qall": _sb(N * Q, "bfloat16"),
-    "qrep": _sb(NW * 16 * H, "bfloat16"), "prod": _sb(NW * 16 * H, "bfloat16"),
+    "nbI": _sb(S, "int32"), "kS": _sb(S, "bfloat16"), "nbbr": _sb(S, "float32"), "qall": _sb(N * QS, "bfloat16"),
+    "kg": _sb(NW * 16 * H, "bfloat16"), "zq": _sb(2 * ZW, "bfloat16"),
     "brX": _sb(256, "int32"), "brF": _sb(256, "float16"), "brT": ("sbuf", [128, 8, 2, 16], "float16"),
     "brY": ("sbuf", [128, 16, 16], "uint16"), "brIn": _sb(256, "uint16"), "ent": _sb(8, "int32"),
-    "lin": _sb(NW * 8, "uint16"), "lout": _sb(NW * 8, "uint16"), "cu": _sb(NW * H, "uint16"), "c0": _sb(Q, "float32"),
-    "dup": _sb(NW * 2 * H, "float16"), "dupT": ("sbuf", [128, NW * B, 2, 16], "float16"),
-    "accin": _sb((N + 1) * Q, "float32"), "rmask": _sb(H, "float32"), "ebig": _sb(144, "bfloat16"),
-    "iI": _sb(H, "int32"), "iP": _sb(16, "int32"), "iD": _sb(160, "int32"), "iB": _sb(128, "int32"), "iJ": _sb(64, "int32"),
-    "iS": _sb(8, "int32"), "t16": _sb(16, "int32"), "evI": _sb(4, "int32"), "cols": _sb(32, "float32"), "m16": _sb(16, "float32"),
-    "mE": _sb(160, "float16"), "mO": _sb(160, "float16"), "gE": _sb(128, "float16"), "gO": _sb(128, "float16"),
-    "c16": _sb(128, "bfloat16"), "c1": _sb(64, "bfloat16"), "boI": _sb(128, "int32"), "bo": _sb(128, "float16"),
-    "s2off": _sb(8, "uint16"), "jj": _sb(16, "float32"), "jM": _sb(64, "float32"),
-    "pX": _sb(64, "float32"), "pK": _sb(64, "float32"), "pKi": _sb(64, "int32"), "pR": _sb(64, "float32"),
-    "plst": _sb(64, "uint16"), "poff": _sb(64 * N, "uint16"), "rr": _sb(NW * H, "float16"),
+    "lin": _sb(NW * 8, "uint16"), "lout": _sb((NW + 1) * 64, "uint16"), "cu": _sb(NW * H, "uint16"),
+    "cf": _sb(NW * 2 * H, "float16"), "cT": ("sbuf", [128, NW * 2, 2, 16], "float16"),
+    "accin": _sb((N + 2) * Q, "float32"), "rmask": _sb(2 * H, "float32"),
+    "iP": _sb(16, "int32"), "iD": _sb(160, "int32"), "iB": _sb(128, "int32"), "iE": _sb(128, "int32"), "iM": _sb(2 * H, "int32"),
+    "iZ": _sb(16 * W, "int32"), "t16": _sb(16, "int32"), "evI": _sb(16, "int32"), "cols": _sb(32, "float32"), "m16": _sb(16, "float32"),
+    "mE": _sb(160, "float16"), "mO": _sb(160, "float16"), "gE": _sb(160, "float16"), "gO": _sb(160, "float16"),
+    "c16": _sb(128, "bfloat16"), "c1": _sb(48 * B, "bfloat16"), "boI": _sb(128, "int32"), "bo": _sb(128, "float16"),
+    "par": _sb(128, "bfloat16"), "half": _sb(2 * H, "bfloat16"), "zF": _sb(16 * W, "float32"), "zoff": _sb(16 * W, "uint16"),
+    "rr": _sb(NW * H, "float16"), "srep": _sb(NW * H, "float32"), "term": _sb(NW * H, "float32"),
+    "rmax": _sb(NW * 2 * H, "float32"), "keep": _sb(NW * 2 * H, "float32"),
 }
-for _n in ("cf", "rmax", "keep", "sel", "srep", "term", "termN"):
-    SCRATCH[_n] = _sb(NW * H, "float32")
 for _n in ("pU0", "pU1", "pP0", "pP1", "pS0", "pS1", "pB"):
     SCRATCH[_n] = ("psum", [128, 512], "float32")
-ROLES = ["v1", "vf", "vtr", "v3", "v4", "v6", "v7", "v8", "s1", "s2", "sr", "sc", "su", "pu", "pp", "ps", "fin",
-         "v20", "v21", "v22", "v23", "v24"]
-SEMAPHORES = (["ldq", "ldbr", "lden", "ldnb", "ldk", "g1", "g2", "g3", "vs", "vI", "vX", "vC", "vY", "vq", "vnb", "pb", "kgo",
+ROLES = ["sn", "sf", "sg0", "sg1", "sg2", "sg3", "vx", "va", "vb", "vc", "vt", "vl", "vy", "vz", "pu", "pp", "ps", "fin"]
+SEMAPHORES = (["ldq", "ldbr", "lden", "ldnb", "ldk", "g1", "g2", "g3", "vs", "vI", "vX", "vC", "vY", "vE", "vnb", "pb", "kgo",
                "loc", "arY", "arH", "st"]
-              + ["%s_%d" % (r, w) for r in ROLES for w in range(W)]
-              + ["sq%d" % n for n in range(NW)] + ["arl%d" % n for n in range(W, NW)]
-              + ["ara%d" % s for s in range(1, N)] + ["arq%d" % s for s in range(1, N)])
+              + ["%s_%d" % (r, w) for r in ROLES for w in range(W)] + ["arl%d" % n for n in range(W, NW)]
+              + ["ara%d" % s for s in range(2, N)] + ["arh%d" % s for s in range(N - 2)] + ["arb0", "arb1"]
+              + ["arq%d" % s for s in range(1, N)])
 
 
 def helper_of(core, cores, topo):
@@ -60,14 +60,22 @@ def bits(m):
 
 def helper_program(g, core, owner, T, topo):
     sem = T.sem
-    g.wait_ge(sem["arH"], bits(topo.mask(T.cores[owner], core)))
+    oc = T.cores[owner]
+    g.wait_ge(sem["arH"], bits(topo.mask(oc, core)))
     total = 0
     for s in range(1, N):
         d = T.cores[(owner + s) % N]
         rid, pid, _ = topo.addr(d)
         m = topo.mask(core, d)
-        g.remote_dma(T.qall[:, s * Q:(s + 1) * Q], T.qall[:, 0:Q], sem["arq%d" % s], sem["loc"], pid, rid, m)
+        g.remote_dma(T.qall[:, s * QS:s * QS + Q], T.qall[:, 0:Q], sem["arq%d" % s], sem["loc"], pid, rid, m)
         total += bits(m)
+    d = T.cores[(owner + 2) % N]
+    rid, pid, _ = topo.addr(d)
+    for s in range(N - 2):
+        g.wait_ge(sem["arh%d" % s], bits(topo.mask(oc, core) & ~topo.mask(oc, T.cores[(owner + 1) % N])))
+        g.remote_dma(T.accin[:, (s + 2) * Q:(s + 3) * Q], T.accin[:, s * Q:(s + 1) * Q], sem["ara%d" % (s + 2)], sem["loc"], pid, rid,
+                     topo.mask(core, d))
+        total += bits(topo.mask(core, d))
     g.wait_ge(sem["loc"], total)
 
 
@@ -91,11 +99,15 @@ def rank_program(g, core, T, topo):
     def sm(role, w):
         return sem["%s_%d" % (role, w)]
 
-    def wv(buf, n):
-        return buf[:, n * H:(n + 1) * H]
+    def wv(buf, n, k=1):
+        return buf[:, n * k * H:(n + 1) * k * H]
 
-    def plist(e):
-        return T.plst[:, 4 * (e + N - 1):4 * (e + N - 1) + B]
+    def slots(order, call):
+        for m in range(-W, NW):
+            for tok in order[max(0, m - NW + len(order))].split():
+                n = m + int(tok[1:])
+                if 0 <= n < NW:
+                    call(tok[0], n)
 
     SY.dma_start(T.brX[:], T.br[:]).then_inc(sem.ldbr, 16)
     SC.dma_start(T.qall[:, 0:Q], T.q[:]).then_inc(sem.ldq, 16)
@@ -106,10 +118,10 @@ def rank_program(g, core, T, topo):
 
     g.iota(T.iP[:], [[-1, 16]], 16, 1).then_inc(sem.g2, 1)
     g.iota(T.iD[:], [[-1, 160]], 16, 1).then_inc(sem.g2, 1)
-    g.iota(T.iI[:], [[1, H]], 0, 0).then_inc(sem.g1, 1)
-    g.iota(T.iJ[:], [[0, 16], [16, 4]], 0, 0).then_inc(sem.g1, 1)
+    g.iota(T.iZ[:], [[H, W], [1, 2], [4, 8]], -Q, 0).then_inc(sem.g1, 1)
     g.iota(T.iB[:], [[-16, 8], [0, 16]], 0, 1).then_inc(sem.g3, 1)
-    g.iota(T.iS[:], [[1, 4], [0, 2]], 0, 0).then_inc(sem.g3, 1)
+    g.iota(T.iE[:], [[0, 64], [-1, 2]], 0, 1).then_inc(sem.g3, 1)
+    g.iota(T.iM[:], [[0, B], [1, 2], [0, 16]], -1, 1).then_inc(sem.g3, 1)
 
     def send(dst, src, rsem):
         g.remote_dma(dst, src, rsem, sem.loc, npid, nrid, nmask)
@@ -129,34 +141,45 @@ def rank_program(g, core, T, topo):
     send(T.brIn[:], T.brY[:], sem.arY)
     g.sem_inc(sem.kgo, 1)
 
+    amask = hmask & ~nmask
+    n2in = bits(topo.mask(helper_of(cores[(rank - 2) % N], cores, topo), core))
+
     def send_acc(s):
         for w in range(W):
-            g.wait_ge(sm("su", w), s + 1)
-        dst = T.accin[:, (s + 1) * Q:(s + 2) * Q]
-        src = T.termN[:, s * Q:(s + 1) * Q]
-        if s == 0:
-            send(dst, src, sem["ara1"])
-        else:
-            g.wait_ge(sem["ara%d" % s], nin)
-            send_sum(dst, [src, T.accin[:, s * Q:(s + 1) * Q]], sem["ara%d" % (s + 1)])
+            g.wait_ge(sm("vt", w), s + 1)
+        srcs = [T.term[:, s * Q:(s + 1) * Q]]
+        if s >= 2:
+            g.wait_ge(sem["ara%d" % s], n2in)
+            srcs.append(T.accin[:, s * Q:(s + 1) * Q])
+        g.remote_dma_fused([RemoteDMATransfer(dst_ids=[DstId(rid=hrid, pnc=hpid)], dma_engine_mask=amask, remote_sem=sem["arh%d" % s],
+                                              srcs=srcs, dsts=[T.accin[:, s * Q:(s + 1) * Q]], alu_op=1 if s >= 2 else 0)],
+                           local_sem=sem.loc)
+        loc[0] += bits(amask)
 
-    for n in range(NW):
+    for n in range(NW - W):
         s, w = divmod(n, W)
-        if s < N - 1:
-            g.wait_ge(sm("v7", w), s + 1)
-            send(T.lin[:, 8 * (n + W):8 * (n + W) + 4], T.lout[:, 8 * n:8 * n + 4], sem["arl%d" % (n + W)])
-        if w == 0 and s >= 1:
+        g.wait_ge(sm("vc", w), B * (s + 1))
+        send(T.lin[:, 8 * (n + W):8 * (n + W) + B], T.lout[:, 64 * (n + 1):64 * (n + 1) + B], sem["arl%d" % (n + W)])
+        if w == SUMS and s >= 1:
             send_acc(s - 1)
-    g.wait_ge(sem["ara%d" % (N - 1)], nin)
+    g.wait_ge(sem["ara%d" % (N - 2)], n2in)
+    for i, ws in enumerate((range(W - 1), [W - 1])):
+        for w in ws:
+            g.wait_ge(sm("vt", w), N - 1)
+        lo, hi = (N - 2) * Q + ws[0] * H, (N - 2) * Q + (ws[-1] + 1) * H
+        send_sum(T.accin[:, lo + 2 * Q:hi + 2 * Q], [T.term[:, lo:hi], T.accin[:, lo:hi]], sem["arb%d" % i])
+    g.wait_ge(sem["ara%d" % (N - 1)], n2in)
     for w in range(W):
-        g.wait_ge(sm("v8", w), N)
+        if w in (0, W - 1):
+            g.wait_ge(sem["arb%d" % (w > 0)], nin)
+        g.wait_ge(sm("vt", w), N)
         n = NW - W + w
-        send_sum(wv(T.accin, n + W), [wv(T.term, n), wv(T.accin, n)], sm("fin", w))
+        send_sum(wv(T.accin, n + 2 * W), [wv(T.term, n), wv(T.accin, n), wv(T.accin, n + W)], sm("fin", w))
     g.wait_ge(sem.loc, loc[0])
 
     for w in range(W):
         SY.wait_ge(sm("fin", w), nin)
-        SY.dma_start(T.y[:, w * H:(w + 1) * H], wv(T.accin, NW + w)).then_inc(sem.st, 16)
+        SY.dma_start(T.y[:, w * H:(w + 1) * H], wv(T.accin, NW + W + w)).then_inc(sem.st, 16)
     SY.wait_ge(sem.st, 16 * W)
 
     vs = [0]
@@ -168,136 +191,115 @@ def rank_program(g, core, T, topo):
     def vw():
         V.wait_ge(sem.vs, vs[0])
 
-    even, odd, pm, pm3, neg, neven, nodd, pmM = (T.cols[:, 4 * i:4 * i + 1] for i in range(8))
+    even, odd, neg, neven, nodd, grp, high, mine = (T.cols[:, 4 * i:4 * i + 1] for i in range(8))
+    p16 = T.iP[:, 0:1]
     v(V.memset(T.rmask[:], 0.0))
-    v(V.memset(T.ebig[:], 0.0))
-    v(V.memset(T.lout[:], 0))
     v(V.memset(T.c16[:], 16.0))
     v(V.memset(T.c1[:], 0.0))
     v(V.memset(neg, -2048.0))
+    v(V.memset(T.qall[:, Q::QS], 0.0))
     V.wait_ge(sem.g2, 2)
     v(V.tensor_scalar(T.t16[:], T.iP[:], 15, None, A.bitwise_and))
-    v(V.tensor_scalar(T.evI[:, 0:1], T.iP[:, 0:1], 4, 1, A.arith_shift_right, A.bitwise_and))
+    v(V.tensor_scalar(T.evI[:, 0:1], p16, 4, 1, A.arith_shift_right, A.bitwise_and))
+    v(V.tensor_scalar(T.evI[:, 4:5], p16, 4, None, A.arith_shift_right))
+    v(V.tensor_scalar(T.evI[:, 8:9], p16, 2, 2, A.arith_shift_right, A.bitwise_and))
+    v(V.tensor_scalar(T.evI[:, 12:13], p16, 7, None, A.bitwise_and))
     vw()
     v(V.tensor_copy(even, T.evI[:, 0:1]))
     v(V.tensor_scalar(odd, T.evI[:, 0:1], -1.0, 1.0, A.mult, A.add))
-    v(V.tensor_copy(pm, T.t16[:, 0:1]))
-    v(V.tensor_scalar(pm3, T.t16[:, 0:1], float(B), None, A.mult))
-    v(V.tensor_scalar(T.m16[:], T.t16[:], 0.0, None, A.is_equal))
-    v(V.memset(T.rmask[:, 0:H:16], -BIG))
-    v(V.memset(T.c1[:, 0:H:16], 1.0))
+    v(V.tensor_scalar(grp, T.evI[:, 4:5], -1.0, None, A.add))
+    v(V.tensor_copy(high, T.evI[:, 8:9]))
     v(V.tensor_scalar(neven, T.evI[:, 0:1], -1.0, None, A.mult))
     v(V.tensor_scalar(nodd, T.evI[:, 0:1], 1.0, None, A.subtract))
-    v(V.tensor_scalar(pmM, T.t16[:, 0:1], -1.0, float(M), A.mult, A.add))
     vw()
     V.tensor_scalar(T.mE[:], T.iD[:], 0.0, even, A.is_equal, A.mult).then_inc(sem.vI, 1)
     V.tensor_scalar(T.mO[:], T.iD[:], 0.0, odd, A.is_equal, A.mult).then_inc(sem.vI, 1)
-    V.wait_ge(sem.g1, 2)
-    for r in range(4):
-        v(V.tensor_scalar(T.jj[:, 4 * r:4 * r + 4], T.iJ[:, 0:4], pm, float(pow(16, r, M)), A.add, A.mult))
-    v(V.tensor_scalar(T.jM[:], T.iJ[:], pmM, float(M), A.is_equal, A.mult))
-    vw()
-    for r in range(4):
-        v(V.tensor_scalar(T.pX[:, 16 * r:16 * r + 16], T.jj[:], float(pow(16, 4 * r + 1 - N, M)), None, A.mult))
+    v(V.tensor_scalar(mine, T.evI[:, 12:13], grp, None, A.is_equal))
+    v(V.tensor_scalar(T.m16[:], T.t16[:], 0.0, None, A.is_equal))
+    v(V.memset(T.rmask[:, 0:2 * H:32], -BIG))
+    v(V.memset(T.c1[:, 0:48 * B:48], 1.0))
     V.wait_ge(sem.ldbr, 16)
     v(V.tensor_scalar(T.brF[:], T.brX[:], -2048.0, None, A.add))
     vw()
     V.transpose(T.brT[:], T.brF[:]).then_inc(sem.vX, 1)
-    v(V.tensor_scalar(T.pK[:], T.pX[:], 1.0 / M, -0.49, A.mult, A.add))
-    v(V.tensor_tensor(T.pR[:], T.pX[:], T.jM[:], A.add))
-    V.wait_ge(sem.g3, 2)
-    v(V.tensor_scalar(T.boI[:], T.iB[:], 4, None, A.arith_shift_right))
-    vw()
-    v(V.tensor_copy(T.pKi[:], T.pK[:]))
+    V.wait_ge(sem.g1, 1)
+    v(V.tensor_scalar(T.zF[:], T.iZ[:], high, mine, A.add, A.mult))
+    V.tensor_scalar(T.gE[:], T.iD[:], 0.0, neven, A.is_equal, A.mult).then_inc(sem.vC, 1)
+    V.tensor_scalar(T.gO[:], T.iD[:], 0.0, nodd, A.is_equal, A.mult).then_inc(sem.vC, 1)
     V.wait_ge(sem.pb, 1)
     for U in range(8):
         V.tensor_scalar(T.brY[:, :, 2 * U:2 * U + 2], T.pB[:, 32 * U:32 * U + 32], 2048.0, None, A.add).then_inc(sem.vY, 1)
-    vw()
-    v(V.tensor_scalar(T.pK[:], T.pKi[:], -float(M), None, A.mult))
-    V.tensor_scalar(T.s2off[:], T.iS[:], pm3, None, A.add).then_inc(sem.vC, 1)
-    V.tensor_scalar(T.bo[:], T.boI[:], 0.0, None, A.is_equal).then_inc(sem.vC, 1)
-    vw()
-    v(V.tensor_tensor(T.pX[:], T.pR[:], T.pK[:], A.add))
-    V.tensor_scalar(T.ebig[:, 15:143:16], T.boI[:, 0:128:16], 0.0, None, A.is_equal).then_inc(sem.vC, 1)
-    V.tensor_scalar(T.gE[:], T.iD[:, 16:144], 0.0, neven, A.is_equal, A.mult).then_inc(sem.vC, 1)
-    vw()
-    v(V.tensor_copy(T.plst[:], T.pX[:]))
-    V.tensor_scalar(T.gO[:], T.iD[:, 16:144], 0.0, nodd, A.is_equal, A.mult).then_inc(sem.vC, 1)
     V.wait_ge(sem.lden, 16)
     for w in range(W):
-        v(V.tensor_copy(T.lin[:, 8 * w:8 * w + B], T.ent[:, B * w:B * w + B]))
+        V.tensor_copy(T.lin[:, 8 * w:8 * w + B], T.ent[:, B * w:B * w + B]).then_inc(sem.vE, 1)
+    V.wait_ge(sem.g3, 3)
+    v(V.tensor_scalar(T.boI[:], T.iB[:], 4, None, A.arith_shift_right))
+    v(V.memset(T.zq[:], 0.0))
     vw()
-    V.tensor_copy(T.poff[:], T.iI[:].indirect(T.plst[:, 4 * N:8 * N])).then_inc(sem.vq, 1)
+    v(V.tensor_scalar(T.zoff[:], T.zF[:], float(Q), None, A.add))
+    V.tensor_scalar(T.bo[:], T.boI[:], 0.0, None, A.is_equal).then_inc(sem.vC, 1)
+    V.tensor_scalar(T.par[:], T.iE[:], 0.0, None, A.is_equal).then_inc(sem.vC, 1)
+    V.tensor_scalar(T.half[:], T.iM[:], 0.0, -OUT, A.is_equal, A.mult).then_inc(sem.vC, 1)
+    V.wait_ge(sem.ldq, 16)
+    vw()
 
     def lst_in(n):
         return T.lin[:, 8 * n:8 * n + B]
 
     def lst_out(n):
-        return T.lout[:, 8 * n:8 * n + B]
+        return T.lout[:, 64 * (n + 1):64 * (n + 1) + B]
 
-    V.wait_ge(sem.ldnb, 16)
-    for w in range(W):
-        v(V.tensor_copy(wv(T.c0, w), T.nbI[:].indirect(lst_in(w))))
-    vw()
-    for w in range(W):
-        V.tensor_copy(wv(T.cf, w), wv(T.c0, w).indirect(plist(N))).then_inc(sm("vf", w), 1)
-        V.tensor_copy(wv(T.cu, w), wv(T.c0, w).indirect(plist(N))).then_inc(sm("v1", w), 1)
-    V.wait_ge(sem.arY, nin)
-    V.tensor_copy(T.nbbr[:, 0:16 * PART1], T.nbI[:].indirect(T.brIn[:, 0:PART1])).then_inc(sem.vnb, 1)
-    V.wait_ge(sem.ldk, 16)
-
-    def term_op(n):
-        s, w = divmod(n, W)
-        V.wait_ge(sm("v7", w), s + 1)
-        V.wait_ge(sm("sc", w), s + 1)
-        V.tensor_tensor(wv(T.term, n), T.kS[:].indirect(lst_out(n)), wv(T.srep, n), A.mult).then_inc(sm("v8", w), 1)
-
-    piece = [0] * NW
+    zdone = [0] * NW
 
     def vec(c, n):
         s, w = divmod(n, W)
         pU, pP = T["pU%d" % (n % 2)], T["pP%d" % (n % 2)]
-        if c == "N" and n >= W:
-            if n == W:
-                V.wait_ge(sem.vnb, 2)
-            V.wait_ge(sem["arl%d" % n], nin)
-            V.tensor_copy(wv(T.cu, n), T.nbbr[:].indirect(lst_in(n))).then_inc(sm("v1", w), 1)
-        elif c == "K":
-            i = piece[n]
-            piece[n] += 1
-            if i == 0:
-                V.wait_ge(sem["sq%d" % n], 1)
-                V.wait_ge(sm("v1", w), s + 1)
-            a0, a1 = CHUNKS[w][i]
-            lo, hi = n * 16 * H + a0 * H, n * 16 * H + a1 * H
-            V.tensor_tensor(T.prod[:, lo:hi], T.kS[:].indirect(T.cu[:, n * H + B * a0:n * H + B * a1]), T.qrep[:, lo:hi],
-                            A.mult).then_inc(sm("v2%d" % i, w), 1)
+        if c == "Z":
+            e = zdone[n]
+            if e == 2:
+                return
+            zdone[n] += 1
+            if s >= 1 and w == 0 and e == 0:
+                V.wait_ge(sem["arq%d" % s], bits(topo.mask(helper_of(cores[(rank - s) % N], cores, topo), core)))
+            lo = (n % 2) * ZW + 16 + e
+            V.tensor_copy(T.zq[:, lo:lo + 64 * H - 8:16], T.qall[:, s * QS:s * QS + Q + 1].indirect(
+                T.zoff[:, 16 * w + 8 * e:16 * w + 8 * e + 8])).then_inc(sm("vz", w), 1)
         elif c == "X":
-            V.wait_ge(sm("s2", w), s + 1)
-            V.transpose(T.dupT[:, B * n:B * n + B], T.dup[:, 2 * n * H:2 * (n + 1) * H]).then_inc(sm("vtr", w), 1)
-        elif c == "T":
-            term_op(n)
+            V.wait_ge(sm("sf", w), 2 * (s + 1))
+            V.transpose(T.cT[:, 2 * n:2 * n + 2], wv(T.cf, n, 2)).then_inc(sm("vx", w), 1)
         elif c == "A":
             V.wait_ge(sm("pu", w), s + 1)
-            V.tensor_tensor_scan(wv(T.rmax, n), T.rmask[:], pU[:, H - 1::-1], 0.0, A.add, A.max).then_inc(sm("v3", w), 1)
+            V.tensor_tensor_scan(wv(T.rmax, n, 2), T.rmask[:], pU[:, 2 * H - 1::-1], 0.0, A.add, A.max).then_inc(sm("va", w), 1)
         elif c == "B":
-            V.wait_ge(sm("v3", w), s + 1)
-            V.tensor_tensor(wv(T.keep, n), wv(T.rmax, n), pU[:, H - 1::-1], A.is_gt).then_inc(sm("v4", w), 1)
+            V.wait_ge(sm("va", w), s + 1)
+            V.tensor_tensor(wv(T.keep, n, 2), wv(T.rmax, n, 2), pU[:, 2 * H - 1::-1], A.is_gt).then_inc(sm("vb", w), 1)
         elif c == "C":
             V.wait_ge(sm("pp", w), s + 1)
-            V.wait_ge(sm("v4", w), s + 1)
-            V.tensor_tensor_scan(wv(T.sel, n), wv(T.keep, n), pP[:, H - 1::-1], 0.0, A.mult, A.add).then_inc(sm("v6", w), 1)
-        elif c == "D":
-            V.wait_ge(sm("v6", w), s + 1)
-            V.tensor_copy(lst_out(n), T.sel[:, n * H + H - 1:n * H:-16]).then_inc(sm("v7", w), 1)
+            V.wait_ge(sm("vb", w), s + 1)
+            for b in range(B):
+                lo, k0, o = 64 * (n + 1) + b, 2 * n * H + 32 * (B - 1 - b), 16 + 48 * b
+                V.tensor_tensor_scan(T.lout[:, lo + 62:lo - 1:-2], T.keep[:, k0:k0 + 32], pP[:, o + 31:o - 1:-1],
+                                     0.0, A.mult, A.add).then_inc(sm("vc", w), 1)
+        elif c == "L":
+            V.wait_ge(sm("va", w), s + 1)
+            for b in range(B):
+                k0 = 2 * (n + 1) * H - 1 - 32 * b
+                V.tensor_scalar(T.rr[:, n * H + 16 * b:n * H + 16 * b + 16], T.m16[:], T.rmax[:, k0:k0 + 1], 0.0,
+                                A.mult, A.max).then_inc(sm("vl", w), 1)
+        elif c == "Y":
+            V.wait_ge(sm("ps", w), s + 1)
+            V.tensor_copy(wv(T.srep, n), T["pS%d" % (n % 2)][:, 0:H]).then_inc(sm("vy", w), 1)
+        else:
+            V.wait_ge(sm("vc", w), B * (s + 1))
+            V.wait_ge(sm("vy", w), s + 1)
+            V.tensor_tensor(wv(T.term, n), T.kS[:].indirect(lst_out(n)), wv(T.srep, n), A.mult).then_inc(sm("vt", w), 1)
 
-    def slots(order, call):
-        for m in range(-W, NW + W):
-            for tok in order[m % len(order)].split():
-                n = m + int(tok[1:])
-                if 0 <= n < NW:
-                    call(tok[0], n)
-
+    for c, n in (("Z", 0), ("Z", 0), ("Z", 1), ("Z", 1)):
+        vec(c, n)
+    V.wait_ge(sem.ldnb, 16)
+    V.wait_ge(sem.arY, nin)
+    V.tensor_copy(T.nbbr[:, 0:16 * PART1], T.nbI[:].indirect(T.brIn[:, 0:PART1])).then_inc(sem.vnb, 1)
+    V.wait_ge(sem.ldk, 16)
     slots(VECTOR, vec)
 
     PE.wait_ge(sem.vI, 2)
@@ -312,90 +314,68 @@ def rank_program(g, core, T, topo):
     def ten(c, n):
         s, w = divmod(n, W)
         pU, pP, pS = T["pU%d" % (n % 2)], T["pP%d" % (n % 2)], T["pS%d" % (n % 2)]
-        if c == "U":
+        if c == "M":
+            PE.matmul(pU[:, 0:2 * H], T.par[:], T.half[:], True, False)
+            PE.wait_ge(sm("vz", w), 2 * (s + 1))
+        elif c == "U":
             i = done[n]
             done[n] += 1
-            PE.wait_ge(sm("v2%d" % i, w), s + 1)
-            for a in range(*CHUNKS[w][i]):
-                lo = n * 16 * H + a * H
-                mm = PE.matmul(pU[:, 0:H], T.ebig[:, 15 - a:143 - a], T.prod[:, lo:lo + H], a == 0, a == 15)
-            if a == 15:
+            PE.wait_ge(sm("sg%d" % i, w), s + 1)
+            for t in range(CHUNKS[i][0] // 2, CHUNKS[i][1] // 2):
+                lo = (n % 2) * ZW + 16 + 128 * t - 2 * (t % 8)
+                mm = PE.matmul(pU[:, 32 * (t // 8):32 * (t // 8) + 32], T.zq[:, lo:lo + 128],
+                               T.kg[:, n * 16 * H + 32 * t:n * 16 * H + 32 * t + 32], False, t == H // 2 - 1)
+            if t == H // 2 - 1:
                 mm.then_inc(sm("pu", w), 1)
-        elif c == "Z":
-            PE.matmul(pP[:, 0:H + 16], T.c16[:], T.c1[:, 0:H + 16], True, False)
         elif c == "P":
-            PE.wait_ge(sm("vtr", w), s + 1)
-            for h, (plus, minus) in enumerate(((T.mE[:, 16:144], T.gE[:]), (T.mO[:, 16:144], T.gO[:]))):
-                PE.matmul(pP[:, 0:H], plus, T.dupT[:, B * n:B * n + B, h, :], False, False)
-                PE.matmul(pP[:, 1:H + 1], minus, T.dupT[:, B * n:B * n + B, h, :], False, False)
-                mm = PE.matmul(pP[:, 16:H + 1:16], plus, T.dupT[:, B * n:B * n + B, h, 15], False, h == 1)
+            PE.wait_ge(sm("vx", w), s + 1)
+            PE.matmul(pP[:, 16:16 + 48 * B], T.c16[:], T.c1[:], True, False)
+            for b, (plus, minus) in enumerate(((T.mE, T.gE), (T.mO, T.gO))):
+                for h in range(2):
+                    x, o = 16 + 16 * (b - h), 16 + 48 * b
+                    PE.matmul(pP[:, o:o + 32], plus[:, x:x + 128], T.cT[:, 2 * n:2 * n + 2, h, :], False, False)
+                    mm = PE.matmul(pP[:, o + 1:o + 33], minus[:, x:x + 128], T.cT[:, 2 * n:2 * n + 2, h, :], False, b + h == 2)
             mm.then_inc(sm("pp", w), 1)
         else:
-            PE.wait_ge(sm("sr", w), B * (s + 1))
+            PE.wait_ge(sm("vl", w), B * (s + 1))
             PE.matmul(pS[:, 0:H], T.bo[:], wv(T.rr, n), True, True).then_inc(sm("ps", w), 1)
 
     slots(TENSOR, ten)
 
-    seen = set()
-
-    def qrep(n):
-        s, w = divmod(n, W)
-        if s >= 1 and s not in seen:
-            seen.add(s)
-            SC.wait_ge(sem["arq%d" % s], bits(topo.mask(helper_of(cores[(rank - s) % N], cores, topo), core)))
-        SC.activation(T.qrep[:, n * 16 * H:(n + 1) * 16 * H], wv(T.qall, n).indirect(T.poff[:, 64 * (N - 1 - s):64 * (N - 1 - s) + H]),
-                      F.Copy).then_inc(sem["sq%d" % n], 1)
-
-    def spread(n):
-        w = n % W
-        SC.activation(T.dup[:, 2 * n * H:2 * (n + 1) * H], wv(T.cf, n).indirect(T.s2off[:, 0:2 * B]), F.Identity,
-                      bias=neg).then_inc(sm("s2", w), 1)
-
-    def unperm(n):
-        s, w = divmod(n, W)
-        if s < N - 1:
-            SC.wait_ge(sm("v8", w), s + 1)
-            if s >= 1:
-                SC.wait_ge(sm("su", w), s)
-            SC.activation(wv(T.termN, n), wv(T.term, n).indirect(plist(s + 1 - N)), F.Copy).then_inc(sm("su", w), 1)
-
-    def score_copy(n):
-        s, w = divmod(n, W)
-        SC.wait_ge(sm("ps", w), s + 1)
-        SC.activation(wv(T.srep, n), T["pS%d" % (n % 2)][:, 0:H], F.Copy).then_inc(sm("sc", w), 1)
-
-    SC.wait_ge(sem.vq, 1)
-    SC.wait_ge(sem.ldq, 16)
-    for n in range(W):
-        qrep(n)
-    SC.wait_ge(sem.vC, 5)
-    for w in range(W):
-        SC.wait_ge(sm("vf", w), 1)
-        spread(w)
-    SC.wait_ge(sem.arY, nin)
-    SC.activation(T.nbbr[:, 16 * PART1:], T.nbI[:].indirect(T.brIn[:, PART1:256]), F.Copy).then_inc(sem.vnb, 1)
+    piece = [0] * NW
 
     def sca(c, n):
         s, w = divmod(n, W)
-        if c == "F" and s >= 1:
+        table = T.nbbr if s else T.nbI
+        if c == "N":
             if n == W:
                 SC.wait_ge(sem.vnb, 2)
-            SC.wait_ge(sem["arl%d" % n], nin)
-            SC.activation(wv(T.cf, n), T.nbbr[:].indirect(lst_in(n)), F.Copy).then_inc(sm("s1", w), 1)
-        elif c == "R" and s >= 1:
-            SC.wait_ge(sm("s1", w), s)
-            spread(n)
-        elif c == "Q" and s >= 1:
-            qrep(n)
-        elif c == "L":
-            SC.wait_ge(sm("v3", w), s + 1)
-            for b in range(B):
-                c = n * H + H - 1 - 16 * b
-                SC.activation(T.rr[:, n * H + 16 * b:n * H + 16 * b + 16], T.m16[:], F.Relu,
-                              scale=T.rmax[:, c:c + 1]).then_inc(sm("sr", w), 1)
-        elif c == "Y":
-            score_copy(n)
-        elif c == "U":
-            unperm(n)
+            if s >= 1:
+                SC.wait_ge(sem["arl%d" % n], nin)
+            SC.activation(wv(T.cu, n), table[:].indirect(lst_in(n)), F.Copy).then_inc(sm("sn", w), 1)
+        elif c == "F":
+            if s >= 1:
+                SC.wait_ge(sm("sf", w), 2 * s)
+            for e in range(2):
+                SC.activation(wv(T.cf, 2 * n + e), table[:].indirect(lst_in(n)), F.Identity, bias=neg).then_inc(sm("sf", w), 1)
+        else:
+            i = piece[n]
+            piece[n] += 1
+            if i == 0:
+                SC.wait_ge(sm("sn", w), s + 1)
+            if s >= 1:
+                SC.wait_ge(sm("sg%d" % i, w), s)
+            lo, hi = CHUNKS[i]
+            SC.activation(T.kg[:, 16 * (n * H + lo):16 * (n * H + hi)], T.kS[:].indirect(T.cu[:, n * H + lo:n * H + hi]),
+                          F.Copy).then_inc(sm("sg%d" % i, w), 1)
 
-    slots(SCALAR, sca)
+    SC.wait_ge(sem.vE, W)
+    SC.wait_ge(sem.vI, 2)
+    SC.wait_ge(sem.ldnb, 16)
+    for n in range(W):
+        sca("N", n)
+        sca("F", n)
+    SC.wait_ge(sem.arY, nin)
+    SC.activation(T.nbbr[:, 16 * PART1:], T.nbI[:].indirect(T.brIn[:, PART1:256]), F.Copy).then_inc(sem.vnb, 1)
+    SC.wait_ge(sem.ldk, 16)
+    slots(SCALAR, lambda c, n: sca(c, n) if c == "G" or n >= W else None)

@@ -3,17 +3,21 @@ from concourse.mybir import AluOpType as A, ActivationFunctionType as F
 
 N, S, Q = 8, 4096, 96
 W = 3
-H = Q // W
-B = H // 16
+HQ = Q // W
+B = 2
+H = 16 * B
 NW = W * N
-QS = Q + 16
+QS = Q
 ZW = 64 * H + 16
-CHUNKS = ((0, 16), (16, 28), (28, 32))
-VECTOR = ("A0 T-1 B0 L0 C0 X1 Z2 Z2 Y0", "A0 T-1 B0 L0 C0 Y0 T0")
-TENSOR = ("P0 M1 U1 S0 U1 U1", "P0 S0")
-SCALAR = ("N1 F1 G1 G1 G1", "")
-PART1 = 144
+CHUNKS = (((0, 16), (16, 28), (28, 32)),) * W
+VPIECE = (9, 9, 9)
+VECTOR = {0: "A0 Y-1 B0 L0 C0 X1 T-1 Z2", NW - W - 1: "A0 Y-1 B0 L0 C0 T-1 Y0 Z2 T0 X1",
+          NW - 2: "A0 Y-1 B0 L0 C0 X1 T-1 W0", NW - 1: "A0 D0 Y-1 B0 T-1 C0 E-1 T0 E0"}
+TENSOR = {0: "M1 U1 U1 U1 S0 P1", NW - W - 1: "S0 M1 U1 U1 U1 P1"}
+SCALAR = {0: "N1 F1 G1 G1 G1", NW - 1: "L0 Y0"}
+TABLE = (((0, 32), (32, 148)), (148, 220), (220, 256))
 SUMS = 0
+FINAL = ((0, 1), (2,))
 BIG = 1.0e9
 OUT = 1048576.0
 
@@ -23,28 +27,28 @@ def _sb(n, d):
 
 
 SCRATCH = {
-    "nbI": _sb(S, "int32"), "kS": _sb(S, "bfloat16"), "nbbr": _sb(S, "float32"), "qall": _sb(N * QS, "bfloat16"),
+    "nbI": _sb(S, "int32"), "kS": _sb(S, "bfloat16"), "nbbr": _sb(S, "float32"), "qall": _sb(N * QS + 16, "bfloat16"),
     "kg": _sb(NW * 16 * H, "bfloat16"), "zq": _sb(2 * ZW, "bfloat16"),
     "brX": _sb(256, "int32"), "brF": _sb(256, "float16"), "brT": ("sbuf", [128, 8, 2, 16], "float16"),
     "brY": ("sbuf", [128, 16, 16], "uint16"), "brIn": _sb(256, "uint16"), "ent": _sb(8, "int32"),
     "lin": _sb(NW * 8, "uint16"), "lout": _sb((NW + 1) * 64, "uint16"), "cu": _sb(NW * H, "uint16"),
-    "cf": _sb(NW * 2 * H, "float16"), "cT": ("sbuf", [128, NW * 2, 2, 16], "float16"),
+    "cf": ("sbuf", [128, NW, 2, H], "float16"), "cT": ("sbuf", [128, NW * 2, 2, 16], "float16"),
     "accin": _sb((N + 2) * Q, "float32"), "rmask": _sb(2 * H, "float32"),
     "iP": _sb(16, "int32"), "iD": _sb(160, "int32"), "iB": _sb(128, "int32"), "iE": _sb(128, "int32"), "iM": _sb(2 * H, "int32"),
-    "iZ": _sb(16 * W, "int32"), "t16": _sb(16, "int32"), "evI": _sb(16, "int32"), "cols": _sb(32, "float32"), "m16": _sb(16, "float32"),
+    "iZ": _sb(B, "int32"), "t16": _sb(16, "int32"), "evI": _sb(16, "int32"), "cols": _sb(32, "float32"), "m16": _sb(16, "float32"),
     "mE": _sb(160, "float16"), "mO": _sb(160, "float16"), "gE": _sb(160, "float16"), "gO": _sb(160, "float16"),
     "c16": _sb(128, "bfloat16"), "c1": _sb(48 * B, "bfloat16"), "boI": _sb(128, "int32"), "bo": _sb(128, "float16"),
-    "par": _sb(128, "bfloat16"), "half": _sb(2 * H, "bfloat16"), "zF": _sb(16 * W, "float32"), "zoff": _sb(16 * W, "uint16"),
-    "rr": _sb(NW * H, "float16"), "srep": _sb(NW * H, "float32"), "term": _sb(NW * H, "float32"),
+    "par": _sb(128, "bfloat16"), "half": _sb(2 * H, "bfloat16"), "zoff": _sb(B, "uint16"),
+    "both": _sb(2 * Q, "float32"), "res": _sb(Q, "float32"), "rr": _sb(NW * H, "float16"), "srep": _sb(NW * H, "float32"), "term": _sb(N * Q + 16, "float32"),
     "rmax": _sb(NW * 2 * H, "float32"), "keep": _sb(NW * 2 * H, "float32"),
 }
-for _n in ("pU0", "pU1", "pP0", "pP1", "pS0", "pS1", "pB"):
+for _n in ("pU0", "pU1", "pP0", "pP1", "pS0", "pS1", "pB0", "pB1"):
     SCRATCH[_n] = ("psum", [128, 512], "float32")
-ROLES = ["sn", "sf", "sg0", "sg1", "sg2", "sg3", "vx", "va", "vb", "vc", "vt", "vl", "vy", "vz", "pu", "pp", "ps", "fin"]
-SEMAPHORES = (["ldq", "ldbr", "lden", "ldnb", "ldk", "g1", "g2", "g3", "vs", "vI", "vX", "vC", "vY", "vE", "vnb", "pb", "kgo",
+ROLES = ["sn", "sf", "sg0", "sg1", "sg2", "sg3", "vx", "va", "vb", "vc", "vt", "vl", "vy", "vz", "pu", "pp", "ps", "fin", "ve"]
+SEMAPHORES = (["z0", "vW", "vF", "s0", "ldq", "ldbr", "lden", "ldnb", "ldk", "g1", "g2", "g3", "vs", "vI", "vX", "vC", "vY", "vE", "vnb", "pb0", "pb1", "kgo",
                "loc", "arY", "arH", "st"]
               + ["%s_%d" % (r, w) for r in ROLES for w in range(W)] + ["arl%d" % n for n in range(W, NW)]
-              + ["ara%d" % s for s in range(2, N)] + ["arh%d" % s for s in range(N - 2)] + ["arb0", "arb1"]
+              + ["ara%d" % s for s in range(2, N)] + ["arh%d" % s for s in range(N - 2)] + ["arb"]
               + ["arq%d" % s for s in range(1, N)])
 
 
@@ -61,6 +65,7 @@ def bits(m):
 def helper_program(g, core, owner, T, topo):
     sem = T.sem
     oc = T.cores[owner]
+    nown = bits(topo.mask(oc, core) & ~topo.mask(oc, T.cores[(owner + 1) % N]))
     g.wait_ge(sem["arH"], bits(topo.mask(oc, core)))
     total = 0
     for s in range(1, N):
@@ -69,10 +74,10 @@ def helper_program(g, core, owner, T, topo):
         m = topo.mask(core, d)
         g.remote_dma(T.qall[:, s * QS:s * QS + Q], T.qall[:, 0:Q], sem["arq%d" % s], sem["loc"], pid, rid, m)
         total += bits(m)
-    d = T.cores[(owner + 2) % N]
-    rid, pid, _ = topo.addr(d)
     for s in range(N - 2):
-        g.wait_ge(sem["arh%d" % s], bits(topo.mask(oc, core) & ~topo.mask(oc, T.cores[(owner + 1) % N])))
+        d = T.cores[(owner + (3 if s == N - 4 else 2)) % N]
+        rid, pid, _ = topo.addr(d)
+        g.wait_ge(sem["arh%d" % s], nown)
         g.remote_dma(T.accin[:, (s + 2) * Q:(s + 3) * Q], T.accin[:, s * Q:(s + 1) * Q], sem["ara%d" % (s + 2)], sem["loc"], pid, rid,
                      topo.mask(core, d))
         total += bits(topo.mask(core, d))
@@ -103,11 +108,16 @@ def rank_program(g, core, T, topo):
         return buf[:, n * k * H:(n + 1) * k * H]
 
     def slots(order, call):
-        for m in range(-W, NW):
-            for tok in order[max(0, m - NW + len(order))].split():
-                n = m + int(tok[1:])
-                if 0 <= n < NW:
-                    call(tok[0], n)
+        made = set()
+        for m in range(-1, NW):
+            for tok in order.get(m, order.get(m % W, order[0])).split():
+                c, n = tok[0], m + int(tok[1:])
+                if 0 <= n < NW and (c in "GU" or (c, n) not in made):
+                    made.add((c, n))
+                    call(c, n)
+
+    def pieces(n):
+        return CHUNKS[n % W]
 
     SY.dma_start(T.brX[:], T.br[:]).then_inc(sem.ldbr, 16)
     SC.dma_start(T.qall[:, 0:Q], T.q[:]).then_inc(sem.ldq, 16)
@@ -118,7 +128,7 @@ def rank_program(g, core, T, topo):
 
     g.iota(T.iP[:], [[-1, 16]], 16, 1).then_inc(sem.g2, 1)
     g.iota(T.iD[:], [[-1, 160]], 16, 1).then_inc(sem.g2, 1)
-    g.iota(T.iZ[:], [[H, W], [1, 2], [4, 8]], -Q, 0).then_inc(sem.g1, 1)
+    g.iota(T.iZ[:], [[1024, B]], 16, 1).then_inc(sem.g1, 1)
     g.iota(T.iB[:], [[-16, 8], [0, 16]], 0, 1).then_inc(sem.g3, 1)
     g.iota(T.iE[:], [[0, 64], [-1, 2]], 0, 1).then_inc(sem.g3, 1)
     g.iota(T.iM[:], [[0, B], [1, 2], [0, 16]], -1, 1).then_inc(sem.g3, 1)
@@ -127,21 +137,16 @@ def rank_program(g, core, T, topo):
         g.remote_dma(dst, src, rsem, sem.loc, npid, nrid, nmask)
         loc[0] += bits(nmask)
 
-    def send_sum(dst, srcs, rsem):
-        g.remote_dma_fused([RemoteDMATransfer(dst_ids=[DstId(rid=nrid, pnc=npid)], dma_engine_mask=nmask, remote_sem=rsem,
-                                              srcs=srcs, dsts=[dst], alu_op=1)], local_sem=sem.loc)
-        loc[0] += bits(nmask)
-
     g.wait_ge(sem.ldq, 16)
     hrid, hpid, _ = topo.addr(hlp)
     hmask = topo.mask(core, hlp)
+    amask = hmask & ~nmask
     g.remote_dma(T.qall[:, 0:Q], T.qall[:, 0:Q], sem.arH, sem.loc, hpid, hrid, hmask)
     loc[0] += bits(hmask)
     g.wait_ge(sem.vY, 8)
     send(T.brIn[:], T.brY[:], sem.arY)
     g.sem_inc(sem.kgo, 1)
 
-    amask = hmask & ~nmask
     n2in = bits(topo.mask(helper_of(cores[(rank - 2) % N], cores, topo), core))
 
     def send_acc(s):
@@ -162,25 +167,20 @@ def rank_program(g, core, T, topo):
         send(T.lin[:, 8 * (n + W):8 * (n + W) + B], T.lout[:, 64 * (n + 1):64 * (n + 1) + B], sem["arl%d" % (n + W)])
         if w == SUMS and s >= 1:
             send_acc(s - 1)
-    g.wait_ge(sem["ara%d" % (N - 2)], n2in)
-    for i, ws in enumerate((range(W - 1), [W - 1])):
-        for w in ws:
-            g.wait_ge(sm("vt", w), N - 1)
-        lo, hi = (N - 2) * Q + ws[0] * H, (N - 2) * Q + (ws[-1] + 1) * H
-        send_sum(T.accin[:, lo + 2 * Q:hi + 2 * Q], [T.term[:, lo:hi], T.accin[:, lo:hi]], sem["arb%d" % i])
-    g.wait_ge(sem["ara%d" % (N - 1)], n2in)
     for w in range(W):
-        if w in (0, W - 1):
-            g.wait_ge(sem["arb%d" % (w > 0)], nin)
-        g.wait_ge(sm("vt", w), N)
-        n = NW - W + w
-        send_sum(wv(T.accin, n + 2 * W), [wv(T.term, n), wv(T.accin, n), wv(T.accin, n + W)], sm("fin", w))
+        g.wait_ge(sm("vt", w), N - 1)
+    send(T.accin[:, N * Q:(N + 1) * Q], T.term[:, (N - 2) * Q:(N - 1) * Q], sem.arb)
+    for i, ws in enumerate(FINAL):
+        g.wait_ge(sm("ve", ws[-1]), 1)
+        lo, hi = ws[0] * HQ, (ws[-1] + 1) * HQ
+        send(T.accin[:, (N + 1) * Q + lo:(N + 1) * Q + hi], T.res[:, lo:hi], sm("fin", i))
     g.wait_ge(sem.loc, loc[0])
 
-    for w in range(W):
-        SY.wait_ge(sm("fin", w), nin)
-        SY.dma_start(T.y[:, w * H:(w + 1) * H], wv(T.accin, NW + W + w)).then_inc(sem.st, 16)
-    SY.wait_ge(sem.st, 16 * W)
+    for i, ws in enumerate(FINAL):
+        SY.wait_ge(sm("fin", i), nin)
+        lo, hi = ws[0] * HQ, (ws[-1] + 1) * HQ
+        SY.dma_start(T.y[:, lo:hi], T.accin[:, (N + 1) * Q + lo:(N + 1) * Q + hi]).then_inc(sem.st, 16)
+    SY.wait_ge(sem.st, 16 * len(FINAL))
 
     vs = [0]
 
@@ -191,30 +191,27 @@ def rank_program(g, core, T, topo):
     def vw():
         V.wait_ge(sem.vs, vs[0])
 
-    even, odd, neg, neven, nodd, grp, high, mine = (T.cols[:, 4 * i:4 * i + 1] for i in range(8))
+    even, odd, neg, neven, nodd, pair, pos = (T.cols[:, 4 * i:4 * i + 1] for i in range(7))
     p16 = T.iP[:, 0:1]
+    V.memset(T.zq[:, 0:ZW // 4], 0.0).then_inc(sem.z0, 1)
     v(V.memset(T.rmask[:], 0.0))
     v(V.memset(T.c16[:], 16.0))
     v(V.memset(T.c1[:], 0.0))
     v(V.memset(neg, -2048.0))
-    v(V.memset(T.qall[:, Q::QS], 0.0))
+    v(V.memset(pos, 2048.0))
     V.wait_ge(sem.g2, 2)
     v(V.tensor_scalar(T.t16[:], T.iP[:], 15, None, A.bitwise_and))
     v(V.tensor_scalar(T.evI[:, 0:1], p16, 4, 1, A.arith_shift_right, A.bitwise_and))
-    v(V.tensor_scalar(T.evI[:, 4:5], p16, 4, None, A.arith_shift_right))
-    v(V.tensor_scalar(T.evI[:, 8:9], p16, 2, 2, A.arith_shift_right, A.bitwise_and))
-    v(V.tensor_scalar(T.evI[:, 12:13], p16, 7, None, A.bitwise_and))
+    v(V.tensor_scalar(T.evI[:, 4:5], p16, 14, None, A.bitwise_and))
     vw()
     v(V.tensor_copy(even, T.evI[:, 0:1]))
     v(V.tensor_scalar(odd, T.evI[:, 0:1], -1.0, 1.0, A.mult, A.add))
-    v(V.tensor_scalar(grp, T.evI[:, 4:5], -1.0, None, A.add))
-    v(V.tensor_copy(high, T.evI[:, 8:9]))
+    v(V.tensor_scalar(pair, T.evI[:, 4:5], 63.0, None, A.mult))
     v(V.tensor_scalar(neven, T.evI[:, 0:1], -1.0, None, A.mult))
     v(V.tensor_scalar(nodd, T.evI[:, 0:1], 1.0, None, A.subtract))
     vw()
     V.tensor_scalar(T.mE[:], T.iD[:], 0.0, even, A.is_equal, A.mult).then_inc(sem.vI, 1)
     V.tensor_scalar(T.mO[:], T.iD[:], 0.0, odd, A.is_equal, A.mult).then_inc(sem.vI, 1)
-    v(V.tensor_scalar(mine, T.evI[:, 12:13], grp, None, A.is_equal))
     v(V.tensor_scalar(T.m16[:], T.t16[:], 0.0, None, A.is_equal))
     v(V.memset(T.rmask[:, 0:2 * H:32], -BIG))
     v(V.memset(T.c1[:, 0:48 * B:48], 1.0))
@@ -223,20 +220,17 @@ def rank_program(g, core, T, topo):
     vw()
     V.transpose(T.brT[:], T.brF[:]).then_inc(sem.vX, 1)
     V.wait_ge(sem.g1, 1)
-    v(V.tensor_scalar(T.zF[:], T.iZ[:], high, mine, A.add, A.mult))
+    v(V.tensor_scalar(T.zoff[:], T.iZ[:], pair, None, A.add))
     V.tensor_scalar(T.gE[:], T.iD[:], 0.0, neven, A.is_equal, A.mult).then_inc(sem.vC, 1)
     V.tensor_scalar(T.gO[:], T.iD[:], 0.0, nodd, A.is_equal, A.mult).then_inc(sem.vC, 1)
-    V.wait_ge(sem.pb, 1)
-    for U in range(8):
-        V.tensor_scalar(T.brY[:, :, 2 * U:2 * U + 2], T.pB[:, 32 * U:32 * U + 32], 2048.0, None, A.add).then_inc(sem.vY, 1)
+    V.wait_ge(sem.pb1, 1)
+    for U in range(4):
+        V.tensor_scalar(T.brY[:, :, 2 * U + 8:2 * U + 10], T.pB1[:, 32 * U:32 * U + 32], 2048.0, None, A.add).then_inc(sem.vY, 1)
     V.wait_ge(sem.lden, 16)
-    for w in range(W):
-        V.tensor_copy(T.lin[:, 8 * w:8 * w + B], T.ent[:, B * w:B * w + B]).then_inc(sem.vE, 1)
+    V.tensor_copy(T.lin[:, 0:6], T.ent[:, 0:6]).then_inc(sem.vE, 1)
     V.wait_ge(sem.g3, 3)
     v(V.tensor_scalar(T.boI[:], T.iB[:], 4, None, A.arith_shift_right))
-    v(V.memset(T.zq[:], 0.0))
     vw()
-    v(V.tensor_scalar(T.zoff[:], T.zF[:], float(Q), None, A.add))
     V.tensor_scalar(T.bo[:], T.boI[:], 0.0, None, A.is_equal).then_inc(sem.vC, 1)
     V.tensor_scalar(T.par[:], T.iE[:], 0.0, None, A.is_equal).then_inc(sem.vC, 1)
     V.tensor_scalar(T.half[:], T.iM[:], 0.0, -OUT, A.is_equal, A.mult).then_inc(sem.vC, 1)
@@ -249,24 +243,17 @@ def rank_program(g, core, T, topo):
     def lst_out(n):
         return T.lout[:, 64 * (n + 1):64 * (n + 1) + B]
 
-    zdone = [0] * NW
-
     def vec(c, n):
         s, w = divmod(n, W)
         pU, pP = T["pU%d" % (n % 2)], T["pP%d" % (n % 2)]
         if c == "Z":
-            e = zdone[n]
-            if e == 2:
-                return
-            zdone[n] += 1
-            if s >= 1 and w == 0 and e == 0:
+            if s >= 1 and w == 0:
                 V.wait_ge(sem["arq%d" % s], bits(topo.mask(helper_of(cores[(rank - s) % N], cores, topo), core)))
-            lo = (n % 2) * ZW + 16 + e
-            V.tensor_copy(T.zq[:, lo:lo + 64 * H - 8:16], T.qall[:, s * QS:s * QS + Q + 1].indirect(
-                T.zoff[:, 16 * w + 8 * e:16 * w + 8 * e + 8])).then_inc(sm("vz", w), 1)
+            V.tensor_copy(T.zq[:, (n % 2) * ZW:(n % 2 + 1) * ZW].indirect(T.zoff[:]),
+                          T.qall[:, n * HQ:n * HQ + H]).then_inc(sm("vz", w), 1)
         elif c == "X":
-            V.wait_ge(sm("sf", w), 2 * (s + 1))
-            V.transpose(T.cT[:, 2 * n:2 * n + 2], wv(T.cf, n, 2)).then_inc(sm("vx", w), 1)
+            V.wait_ge(sm("sf", w) if s else sem.vF, 2 * (s or W))
+            V.transpose(T.cT[:, 2 * n:2 * n + 2], T.cf[:, n]).then_inc(sm("vx", w), 1)
         elif c == "A":
             V.wait_ge(sm("pu", w), s + 1)
             V.tensor_tensor_scan(wv(T.rmax, n, 2), T.rmask[:], pU[:, 2 * H - 1::-1], 0.0, A.add, A.max).then_inc(sm("va", w), 1)
@@ -280,6 +267,27 @@ def rank_program(g, core, T, topo):
                 lo, k0, o = 64 * (n + 1) + b, 2 * n * H + 32 * (B - 1 - b), 16 + 48 * b
                 V.tensor_tensor_scan(T.lout[:, lo + 62:lo - 1:-2], T.keep[:, k0:k0 + 32], pP[:, o + 31:o - 1:-1],
                                      0.0, A.mult, A.add).then_inc(sm("vc", w), 1)
+        elif c == "W":
+            V.wait_ge(sem["ara%d" % (N - 2)], bits(topo.mask(helper_of(cores[(rank - 3) % N], cores, topo), core)))
+            V.wait_ge(sem["ara%d" % (N - 1)], n2in)
+            V.tensor_tensor(T.both[:, 0:Q], T.accin[:, (N - 2) * Q:(N - 1) * Q], T.accin[:, (N - 1) * Q:N * Q], A.add).then_inc(sem.vW, 1)
+        elif c == "D":
+            V.wait_ge(sem.vW, 1)
+            V.wait_ge(sem.arb, nin)
+            V.tensor_tensor(T.both[:, Q:], T.both[:, 0:Q], T.accin[:, N * Q:(N + 1) * Q], A.add).then_inc(sem.vW, 1)
+        elif c == "E":
+            ws = [x for x in FINAL if x[-1] == w][0]
+            lo, hi = ws[0] * HQ, (w + 1) * HQ
+            V.wait_ge(sem.vW, 2)
+            V.wait_ge(sm("vt", w), N)
+            V.tensor_tensor(T.res[:, lo:hi], T.term[:, (N - 1) * Q + lo:(N - 1) * Q + hi], T.both[:, Q + lo:Q + hi],
+                            A.add).then_inc(sm("ve", w), 1)
+        elif c == "G":
+            i = VPIECE[w]
+            lo, hi = pieces(n)[i]
+            V.wait_ge(sm("sn", w) if s else sem.s0, max(s, 1))
+            V.tensor_copy(T.kg[:, 16 * (n * H + lo):16 * (n * H + hi)],
+                          T.kS[:].indirect(T.cu[:, n * H + lo:n * H + hi])).then_inc(sm("sg%d" % i, w), 1)
         elif c == "L":
             V.wait_ge(sm("va", w), s + 1)
             for b in range(B):
@@ -292,22 +300,34 @@ def rank_program(g, core, T, topo):
         else:
             V.wait_ge(sm("vc", w), B * (s + 1))
             V.wait_ge(sm("vy", w), s + 1)
-            V.tensor_tensor(wv(T.term, n), T.kS[:].indirect(lst_out(n)), wv(T.srep, n), A.mult).then_inc(sm("vt", w), 1)
+            if n >= 1:
+                V.wait_ge(sm("vt", (n - 1) % W), (n - 1) // W + 1)
+            V.tensor_tensor(T.term[:, n * HQ:n * HQ + H], T.kS[:].indirect(lst_out(n)), wv(T.srep, n), A.mult).then_inc(sm("vt", w), 1)
 
-    for c, n in (("Z", 0), ("Z", 0), ("Z", 1), ("Z", 1)):
-        vec(c, n)
+    V.wait_ge(sem.z0, 8)
+    for n in range(2):
+        vec("Z", n)
+    V.wait_ge(sem.vE, 1)
     V.wait_ge(sem.ldnb, 16)
+    for n in range(W):
+        for e in range(2):
+            V.tensor_scalar(T.cf[:, n, e, :], T.nbI[:].indirect(T.lin[:, B * n:B * n + B]), -2048.0, None, A.add).then_inc(sem.vF, 1)
     V.wait_ge(sem.arY, nin)
-    V.tensor_copy(T.nbbr[:, 0:16 * PART1], T.nbI[:].indirect(T.brIn[:, 0:PART1])).then_inc(sem.vnb, 1)
+    for lo, hi in TABLE[0]:
+        V.tensor_copy(T.nbbr[:, 16 * lo:16 * hi], T.nbI[:].indirect(T.brIn[:, lo:hi])).then_inc(sem.vnb, 1)
+        if lo == 0:
+            vec("X", 0)
     V.wait_ge(sem.ldk, 16)
-    slots(VECTOR, vec)
+    slots(VECTOR, lambda c, n: vec(c, n) if (c, n) not in (("Z", 0), ("Z", 1), ("X", 0)) else None)
 
     PE.wait_ge(sem.vI, 2)
     PE.wait_ge(sem.vX, 1)
-    PE.matmul(T.pB[:, 0:256:2], T.mE[:, 16:144], T.brT[:, :, 0, :], True, False)
-    PE.matmul(T.pB[:, 0:256:2], T.mE[:, 0:128], T.brT[:, :, 1, :], False, True)
-    PE.matmul(T.pB[:, 1:256:2], T.mO[:, 32:160], T.brT[:, :, 0, :], True, False)
-    PE.matmul(T.pB[:, 1:256:2], T.mO[:, 16:144], T.brT[:, :, 1, :], False, True).then_inc(sem.pb, 1)
+    for i in range(2):
+        pB, us = T["pB%d" % i], slice(4 * i, 4 * i + 4)
+        PE.matmul(pB[:, 0:128:2], T.mE[:, 16:144], T.brT[:, us, 0, :], True, False)
+        PE.matmul(pB[:, 0:128:2], T.mE[:, 0:128], T.brT[:, us, 1, :], False, True)
+        PE.matmul(pB[:, 1:128:2], T.mO[:, 32:160], T.brT[:, us, 0, :], True, False)
+        PE.matmul(pB[:, 1:128:2], T.mO[:, 16:144], T.brT[:, us, 1, :], False, True).then_inc(sem["pb%d" % i], 1)
     PE.wait_ge(sem.vC, 5)
     done = [0] * NW
 
@@ -315,20 +335,24 @@ def rank_program(g, core, T, topo):
         s, w = divmod(n, W)
         pU, pP, pS = T["pU%d" % (n % 2)], T["pP%d" % (n % 2)], T["pS%d" % (n % 2)]
         if c == "M":
+            if n >= 2:
+                PE.wait_ge(sm("vb", (n - 2) % W), (n - 2) // W + 1)
             PE.matmul(pU[:, 0:2 * H], T.par[:], T.half[:], True, False)
-            PE.wait_ge(sm("vz", w), 2 * (s + 1))
+            PE.wait_ge(sm("vz", w), s + 1)
         elif c == "U":
             i = done[n]
             done[n] += 1
             PE.wait_ge(sm("sg%d" % i, w), s + 1)
-            for t in range(CHUNKS[i][0] // 2, CHUNKS[i][1] // 2):
+            for t in range(pieces(n)[i][0] // 2, pieces(n)[i][1] // 2):
                 lo = (n % 2) * ZW + 16 + 128 * t - 2 * (t % 8)
                 mm = PE.matmul(pU[:, 32 * (t // 8):32 * (t // 8) + 32], T.zq[:, lo:lo + 128],
-                               T.kg[:, n * 16 * H + 32 * t:n * 16 * H + 32 * t + 32], False, t == H // 2 - 1)
-            if t == H // 2 - 1:
+                               T.kg[:, n * 16 * H + 32 * t:n * 16 * H + 32 * t + 32], False, t == HQ // 2 - 1)
+            if t == HQ // 2 - 1:
                 mm.then_inc(sm("pu", w), 1)
         elif c == "P":
             PE.wait_ge(sm("vx", w), s + 1)
+            if n >= 2:
+                PE.wait_ge(sm("vc", (n - 2) % W), B * ((n - 2) // W + 1))
             PE.matmul(pP[:, 16:16 + 48 * B], T.c16[:], T.c1[:], True, False)
             for b, (plus, minus) in enumerate(((T.mE, T.gE), (T.mO, T.gO))):
                 for h in range(2):
@@ -346,36 +370,55 @@ def rank_program(g, core, T, topo):
 
     def sca(c, n):
         s, w = divmod(n, W)
-        table = T.nbbr if s else T.nbI
         if c == "N":
             if n == W:
-                SC.wait_ge(sem.vnb, 2)
-            if s >= 1:
-                SC.wait_ge(sem["arl%d" % n], nin)
-            SC.activation(wv(T.cu, n), table[:].indirect(lst_in(n)), F.Copy).then_inc(sm("sn", w), 1)
+                table(*TABLE[2])
+                SC.wait_ge(sem.vnb, 4)
+            SC.wait_ge(sem["arl%d" % n], nin)
+            SC.activation(wv(T.cu, n), T.nbbr[:].indirect(lst_in(n)), F.Copy).then_inc(sm("sn", w), 1)
         elif c == "F":
-            if s >= 1:
-                SC.wait_ge(sm("sf", w), 2 * s)
+            if s >= 2:
+                SC.wait_ge(sm("sf", w), 2 * (s - 1))
             for e in range(2):
-                SC.activation(wv(T.cf, 2 * n + e), table[:].indirect(lst_in(n)), F.Identity, bias=neg).then_inc(sm("sf", w), 1)
+                SC.activation(T.cf[:, n, e, :], T.nbbr[:].indirect(lst_in(n)), F.Identity, bias=neg).then_inc(sm("sf", w), 1)
+        elif c == "L":
+            SC.wait_ge(sm("va", w), s + 1)
+            for b in range(B):
+                k0 = 2 * (n + 1) * H - 1 - 32 * b
+                SC.activation(T.rr[:, n * H + 16 * b:n * H + 16 * b + 16], T.m16[:], F.Relu,
+                              scale=T.rmax[:, k0:k0 + 1]).then_inc(sm("vl", w), 1)
+        elif c == "Y":
+            SC.wait_ge(sm("ps", w), s + 1)
+            SC.activation(wv(T.srep, n), T["pS%d" % (n % 2)][:, 0:H], F.Copy).then_inc(sm("vy", w), 1)
         else:
             i = piece[n]
             piece[n] += 1
-            if i == 0:
-                SC.wait_ge(sm("sn", w), s + 1)
+            if i == VPIECE[w]:
+                return
+            if i == 0 and s >= 1:
+                SC.wait_ge(sm("sn", w), s)
             if s >= 1:
                 SC.wait_ge(sm("sg%d" % i, w), s)
-            lo, hi = CHUNKS[i]
+            lo, hi = pieces(n)[i]
             SC.activation(T.kg[:, 16 * (n * H + lo):16 * (n * H + hi)], T.kS[:].indirect(T.cu[:, n * H + lo:n * H + hi]),
                           F.Copy).then_inc(sm("sg%d" % i, w), 1)
 
-    SC.wait_ge(sem.vE, W)
+    def table(lo, hi):
+        SC.activation(T.nbbr[:, 16 * lo:16 * hi], T.nbI[:].indirect(T.brIn[:, lo:hi]), F.Copy).then_inc(sem.vnb, 1)
+
+    SC.wait_ge(sem.z0, 1)
+    for i in range(1, 8):
+        SC.activation(T.zq[:, i * ZW // 4:(i + 1) * ZW // 4], T.zq[:, 0:ZW // 4], F.Copy).then_inc(sem.z0, 1)
+        if i == 4:
+            SC.wait_ge(sem.pb0, 1)
+            for U in range(4):
+                SC.activation(T.brY[:, :, 2 * U:2 * U + 2], T.pB0[:, 32 * U:32 * U + 32], F.Identity, bias=pos).then_inc(sem.vY, 1)
+    SC.wait_ge(sem.vE, 1)
     SC.wait_ge(sem.vI, 2)
     SC.wait_ge(sem.ldnb, 16)
-    for n in range(W):
-        sca("N", n)
-        sca("F", n)
+    SC.activation(T.cu[:, 0:Q], T.nbI[:].indirect(T.lin[:, 0:B * W]), F.Copy).then_inc(sem.s0, 1)
     SC.wait_ge(sem.arY, nin)
-    SC.activation(T.nbbr[:, 16 * PART1:], T.nbI[:].indirect(T.brIn[:, PART1:256]), F.Copy).then_inc(sem.vnb, 1)
+    table(*TABLE[1])
+    SC.wait_ge(sem.s0, 1)
     SC.wait_ge(sem.ldk, 16)
-    slots(SCALAR, lambda c, n: sca(c, n) if c == "G" or n >= W else None)
+    slots(SCALAR, lambda c, n: sca(c, n) if c not in "NF" or n >= W else None)

from concourse.bass import DstId, RemoteDMATransfer
from concourse.mybir import AluOpType as A, ActivationFunctionType as F

N, S, Q = 8, 4096, 96
W = 3
HQ = Q // W
B = 2
H = 16 * B
NW = W * N
QS = Q
ZW = 64 * H + 16
CHUNKS = (((0, 16), (16, 28), (28, 32)),) * W
VPIECE = (9, 9, 9)
VECTOR = {0: "A0 Y-1 B0 L0 C0 X1 T-1 Z2", NW - W - 1: "A0 Y-1 B0 L0 C0 T-1 Y0 Z2 T0 X1",
          NW - 2: "A0 Y-1 B0 L0 C0 X1 T-1 W0", NW - 1: "A0 D0 Y-1 B0 T-1 C0 E-1 T0 E0"}
TENSOR = {0: "M1 U1 U1 U1 S0 P1", NW - W - 1: "S0 M1 U1 U1 U1 P1"}
SCALAR = {0: "N1 F1 G1 G1 G1", NW - 1: "L0 Y0"}
TABLE = (((0, 32), (32, 148)), (148, 220), (220, 256))
SUMS = 0
FINAL = ((0, 1), (2,))
BIG = 1.0e9
OUT = 1048576.0


def _sb(n, d):
    return ("sbuf", [128, n], d)


SCRATCH = {
    "nbI": _sb(S, "int32"), "kS": _sb(S, "bfloat16"), "nbbr": _sb(S, "float32"), "qall": _sb(N * QS + 16, "bfloat16"),
    "kg": _sb(NW * 16 * H, "bfloat16"), "zq": _sb(2 * ZW, "bfloat16"),
    "brX": _sb(256, "int32"), "brF": _sb(256, "float16"), "brT": ("sbuf", [128, 8, 2, 16], "float16"),
    "brY": ("sbuf", [128, 16, 16], "uint16"), "brIn": _sb(256, "uint16"), "ent": _sb(8, "int32"),
    "lin": _sb(NW * 8, "uint16"), "lout": _sb((NW + 1) * 64, "uint16"), "cu": _sb(NW * H, "uint16"),
    "cf": ("sbuf", [128, NW, 2, H], "float16"), "cT": ("sbuf", [128, NW * 2, 2, 16], "float16"),
    "accin": _sb((N + 2) * Q, "float32"), "rmask": _sb(2 * H, "float32"),
    "iP": _sb(16, "int32"), "iD": _sb(160, "int32"), "iB": _sb(128, "int32"), "iE": _sb(128, "int32"), "iM": _sb(2 * H, "int32"),
    "iZ": _sb(B, "int32"), "t16": _sb(16, "int32"), "evI": _sb(16, "int32"), "cols": _sb(32, "float32"), "m16": _sb(16, "float32"),
    "mE": _sb(160, "float16"), "mO": _sb(160, "float16"), "gE": _sb(160, "float16"), "gO": _sb(160, "float16"),
    "c16": _sb(128, "bfloat16"), "c1": _sb(48 * B, "bfloat16"), "boI": _sb(128, "int32"), "bo": _sb(128, "float16"),
    "par": _sb(128, "bfloat16"), "half": _sb(2 * H, "bfloat16"), "zoff": _sb(B, "uint16"),
    "both": _sb(2 * Q, "float32"), "res": _sb(Q, "float32"), "rr": _sb(NW * H, "float16"), "srep": _sb(NW * H, "float32"), "term": _sb(N * Q + 16, "float32"),
    "rmax": _sb(NW * 2 * H, "float32"), "keep": _sb(NW * 2 * H, "float32"),
}
for _n in ("pU0", "pU1", "pP0", "pP1", "pS0", "pS1", "pB0", "pB1"):
    SCRATCH[_n] = ("psum", [128, 512], "float32")
ROLES = ["sn", "sf", "sg0", "sg1", "sg2", "sg3", "vx", "va", "vb", "vc", "vt", "vl", "vy", "vz", "pu", "pp", "ps", "fin", "ve"]
SEMAPHORES = (["z0", "vW", "vF", "s0", "ldq", "ldbr", "lden", "ldnb", "ldk", "g1", "g2", "g3", "vs", "vI", "vX", "vC", "vY", "vE", "vnb", "pb0", "pb1", "kgo",
               "loc", "arY", "arH", "st"]
              + ["%s_%d" % (r, w) for r in ROLES for w in range(W)] + ["arl%d" % n for n in range(W, NW)]
              + ["ara%d" % s for s in range(2, N)] + ["arh%d" % s for s in range(N - 2)] + ["arb"]
              + ["arq%d" % s for s in range(1, N)])


def helper_of(core, cores, topo):
    ok = [c for c in topo.cores_of(core) if c not in cores and all(topo.may_write(c, d) for d in cores)]
    same = [c for c in ok if topo.die(c) == topo.die(core)]
    return (same or ok)[0]


def bits(m):
    return bin(m).count("1")


def helper_program(g, core, owner, T, topo):
    sem = T.sem
    oc = T.cores[owner]
    nown = bits(topo.mask(oc, core) & ~topo.mask(oc, T.cores[(owner + 1) % N]))
    g.wait_ge(sem["arH"], bits(topo.mask(oc, core)))
    total = 0
    for s in range(1, N):
        d = T.cores[(owner + s) % N]
        rid, pid, _ = topo.addr(d)
        m = topo.mask(core, d)
        g.remote_dma(T.qall[:, s * QS:s * QS + Q], T.qall[:, 0:Q], sem["arq%d" % s], sem["loc"], pid, rid, m)
        total += bits(m)
    for s in range(N - 2):
        d = T.cores[(owner + (3 if s == N - 4 else 2)) % N]
        rid, pid, _ = topo.addr(d)
        g.wait_ge(sem["arh%d" % s], nown)
        g.remote_dma(T.accin[:, (s + 2) * Q:(s + 3) * Q], T.accin[:, s * Q:(s + 1) * Q], sem["ara%d" % (s + 2)], sem["loc"], pid, rid,
                     topo.mask(core, d))
        total += bits(topo.mask(core, d))
    g.wait_ge(sem["loc"], total)


def rank_program(g, core, T, topo):
    cores = list(T.cores)
    rank = T.rank_of(core)
    if rank is None:
        for r, c in enumerate(cores):
            if helper_of(c, cores, topo) == core:
                helper_program(g, core, r, T, topo)
        return
    sem = T.sem
    V, SC, PE, SY = g.vector, g.scalar, g.tensor, g.sync
    nxt, prv = cores[(rank + 1) % N], cores[(rank - 1) % N]
    nrid, npid, _ = topo.addr(nxt)
    nmask = topo.mask(core, nxt)
    nin = bits(topo.mask(prv, core))
    hlp = helper_of(core, cores, topo)
    loc = [0]

    def sm(role, w):
        return sem["%s_%d" % (role, w)]

    def wv(buf, n, k=1):
        return buf[:, n * k * H:(n + 1) * k * H]

    def slots(order, call):
        made = set()
        for m in range(-1, NW):
            for tok in order.get(m, order.get(m % W, order[0])).split():
                c, n = tok[0], m + int(tok[1:])
                if 0 <= n < NW and (c in "GU" or (c, n) not in made):
                    made.add((c, n))
                    call(c, n)

    def pieces(n):
        return CHUNKS[n % W]

    SY.dma_start(T.brX[:], T.br[:]).then_inc(sem.ldbr, 16)
    SC.dma_start(T.qall[:, 0:Q], T.q[:]).then_inc(sem.ldq, 16)
    SC.dma_start(T.ent[:, 0:6], T.entry[:]).then_inc(sem.lden, 16)
    SY.dma_start(T.nbI[:], T.nb[:]).then_inc(sem.ldnb, 16)
    SY.wait_ge(sem.kgo, 1)
    SY.dma_start(T.kS[:], T.k[:]).then_inc(sem.ldk, 16)

    g.iota(T.iP[:], [[-1, 16]], 16, 1).then_inc(sem.g2, 1)
    g.iota(T.iD[:], [[-1, 160]], 16, 1).then_inc(sem.g2, 1)
    g.iota(T.iZ[:], [[1024, B]], 16, 1).then_inc(sem.g1, 1)
    g.iota(T.iB[:], [[-16, 8], [0, 16]], 0, 1).then_inc(sem.g3, 1)
    g.iota(T.iE[:], [[0, 64], [-1, 2]], 0, 1).then_inc(sem.g3, 1)
    g.iota(T.iM[:], [[0, B], [1, 2], [0, 16]], -1, 1).then_inc(sem.g3, 1)

    def send(dst, src, rsem):
        g.remote_dma(dst, src, rsem, sem.loc, npid, nrid, nmask)
        loc[0] += bits(nmask)

    g.wait_ge(sem.ldq, 16)
    hrid, hpid, _ = topo.addr(hlp)
    hmask = topo.mask(core, hlp)
    amask = hmask & ~nmask
    g.remote_dma(T.qall[:, 0:Q], T.qall[:, 0:Q], sem.arH, sem.loc, hpid, hrid, hmask)
    loc[0] += bits(hmask)
    g.wait_ge(sem.vY, 8)
    send(T.brIn[:], T.brY[:], sem.arY)
    g.sem_inc(sem.kgo, 1)

    n2in = bits(topo.mask(helper_of(cores[(rank - 2) % N], cores, topo), core))

    def send_acc(s):
        for w in range(W):
            g.wait_ge(sm("vt", w), s + 1)
        srcs = [T.term[:, s * Q:(s + 1) * Q]]
        if s >= 2:
            g.wait_ge(sem["ara%d" % s], n2in)
            srcs.append(T.accin[:, s * Q:(s + 1) * Q])
        g.remote_dma_fused([RemoteDMATransfer(dst_ids=[DstId(rid=hrid, pnc=hpid)], dma_engine_mask=amask, remote_sem=sem["arh%d" % s],
                                              srcs=srcs, dsts=[T.accin[:, s * Q:(s + 1) * Q]], alu_op=1 if s >= 2 else 0)],
                           local_sem=sem.loc)
        loc[0] += bits(amask)

    for n in range(NW - W):
        s, w = divmod(n, W)
        g.wait_ge(sm("vc", w), B * (s + 1))
        send(T.lin[:, 8 * (n + W):8 * (n + W) + B], T.lout[:, 64 * (n + 1):64 * (n + 1) + B], sem["arl%d" % (n + W)])
        if w == SUMS and s >= 1:
            send_acc(s - 1)
    for w in range(W):
        g.wait_ge(sm("vt", w), N - 1)
    send(T.accin[:, N * Q:(N + 1) * Q], T.term[:, (N - 2) * Q:(N - 1) * Q], sem.arb)
    for i, ws in enumerate(FINAL):
        g.wait_ge(sm("ve", ws[-1]), 1)
        lo, hi = ws[0] * HQ, (ws[-1] + 1) * HQ
        send(T.accin[:, (N + 1) * Q + lo:(N + 1) * Q + hi], T.res[:, lo:hi], sm("fin", i))
    g.wait_ge(sem.loc, loc[0])

    for i, ws in enumerate(FINAL):
        SY.wait_ge(sm("fin", i), nin)
        lo, hi = ws[0] * HQ, (ws[-1] + 1) * HQ
        SY.dma_start(T.y[:, lo:hi], T.accin[:, (N + 1) * Q + lo:(N + 1) * Q + hi]).then_inc(sem.st, 16)
    SY.wait_ge(sem.st, 16 * len(FINAL))

    vs = [0]

    def v(ins):
        ins.then_inc(sem.vs, 1)
        vs[0] += 1

    def vw():
        V.wait_ge(sem.vs, vs[0])

    even, odd, neg, neven, nodd, pair, pos = (T.cols[:, 4 * i:4 * i + 1] for i in range(7))
    p16 = T.iP[:, 0:1]
    V.memset(T.zq[:, 0:ZW // 4], 0.0).then_inc(sem.z0, 1)
    v(V.memset(T.rmask[:], 0.0))
    v(V.memset(T.c16[:], 16.0))
    v(V.memset(T.c1[:], 0.0))
    v(V.memset(neg, -2048.0))
    v(V.memset(pos, 2048.0))
    V.wait_ge(sem.g2, 2)
    v(V.tensor_scalar(T.t16[:], T.iP[:], 15, None, A.bitwise_and))
    v(V.tensor_scalar(T.evI[:, 0:1], p16, 4, 1, A.arith_shift_right, A.bitwise_and))
    v(V.tensor_scalar(T.evI[:, 4:5], p16, 14, None, A.bitwise_and))
    vw()
    v(V.tensor_copy(even, T.evI[:, 0:1]))
    v(V.tensor_scalar(odd, T.evI[:, 0:1], -1.0, 1.0, A.mult, A.add))
    v(V.tensor_scalar(pair, T.evI[:, 4:5], 63.0, None, A.mult))
    v(V.tensor_scalar(neven, T.evI[:, 0:1], -1.0, None, A.mult))
    v(V.tensor_scalar(nodd, T.evI[:, 0:1], 1.0, None, A.subtract))
    vw()
    V.tensor_scalar(T.mE[:], T.iD[:], 0.0, even, A.is_equal, A.mult).then_inc(sem.vI, 1)
    V.tensor_scalar(T.mO[:], T.iD[:], 0.0, odd, A.is_equal, A.mult).then_inc(sem.vI, 1)
    v(V.tensor_scalar(T.m16[:], T.t16[:], 0.0, None, A.is_equal))
    v(V.memset(T.rmask[:, 0:2 * H:32], -BIG))
    v(V.memset(T.c1[:, 0:48 * B:48], 1.0))
    V.wait_ge(sem.ldbr, 16)
    v(V.tensor_scalar(T.brF[:], T.brX[:], -2048.0, None, A.add))
    vw()
    V.transpose(T.brT[:], T.brF[:]).then_inc(sem.vX, 1)
    V.wait_ge(sem.g1, 1)
    v(V.tensor_scalar(T.zoff[:], T.iZ[:], pair, None, A.add))
    V.tensor_scalar(T.gE[:], T.iD[:], 0.0, neven, A.is_equal, A.mult).then_inc(sem.vC, 1)
    V.tensor_scalar(T.gO[:], T.iD[:], 0.0, nodd, A.is_equal, A.mult).then_inc(sem.vC, 1)
    V.wait_ge(sem.pb1, 1)
    for U in range(4):
        V.tensor_scalar(T.brY[:, :, 2 * U + 8:2 * U + 10], T.pB1[:, 32 * U:32 * U + 32], 2048.0, None, A.add).then_inc(sem.vY, 1)
    V.wait_ge(sem.lden, 16)
    V.tensor_copy(T.lin[:, 0:6], T.ent[:, 0:6]).then_inc(sem.vE, 1)
    V.wait_ge(sem.g3, 3)
    v(V.tensor_scalar(T.boI[:], T.iB[:], 4, None, A.arith_shift_right))
    vw()
    V.tensor_scalar(T.bo[:], T.boI[:], 0.0, None, A.is_equal).then_inc(sem.vC, 1)
    V.tensor_scalar(T.par[:], T.iE[:], 0.0, None, A.is_equal).then_inc(sem.vC, 1)
    V.tensor_scalar(T.half[:], T.iM[:], 0.0, -OUT, A.is_equal, A.mult).then_inc(sem.vC, 1)
    V.wait_ge(sem.ldq, 16)
    vw()

    def lst_in(n):
        return T.lin[:, 8 * n:8 * n + B]

    def lst_out(n):
        return T.lout[:, 64 * (n + 1):64 * (n + 1) + B]

    def vec(c, n):
        s, w = divmod(n, W)
        pU, pP = T["pU%d" % (n % 2)], T["pP%d" % (n % 2)]
        if c == "Z":
            if s >= 1 and w == 0:
                V.wait_ge(sem["arq%d" % s], bits(topo.mask(helper_of(cores[(rank - s) % N], cores, topo), core)))
            V.tensor_copy(T.zq[:, (n % 2) * ZW:(n % 2 + 1) * ZW].indirect(T.zoff[:]),
                          T.qall[:, n * HQ:n * HQ + H]).then_inc(sm("vz", w), 1)
        elif c == "X":
            V.wait_ge(sm("sf", w) if s else sem.vF, 2 * (s or W))
            V.transpose(T.cT[:, 2 * n:2 * n + 2], T.cf[:, n]).then_inc(sm("vx", w), 1)
        elif c == "A":
            V.wait_ge(sm("pu", w), s + 1)
            V.tensor_tensor_scan(wv(T.rmax, n, 2), T.rmask[:], pU[:, 2 * H - 1::-1], 0.0, A.add, A.max).then_inc(sm("va", w), 1)
        elif c == "B":
            V.wait_ge(sm("va", w), s + 1)
            V.tensor_tensor(wv(T.keep, n, 2), wv(T.rmax, n, 2), pU[:, 2 * H - 1::-1], A.is_gt).then_inc(sm("vb", w), 1)
        elif c == "C":
            V.wait_ge(sm("pp", w), s + 1)
            V.wait_ge(sm("vb", w), s + 1)
            for b in range(B):
                lo, k0, o = 64 * (n + 1) + b, 2 * n * H + 32 * (B - 1 - b), 16 + 48 * b
                V.tensor_tensor_scan(T.lout[:, lo + 62:lo - 1:-2], T.keep[:, k0:k0 + 32], pP[:, o + 31:o - 1:-1],
                                     0.0, A.mult, A.add).then_inc(sm("vc", w), 1)
        elif c == "W":
            V.wait_ge(sem["ara%d" % (N - 2)], bits(topo.mask(helper_of(cores[(rank - 3) % N], cores, topo), core)))
            V.wait_ge(sem["ara%d" % (N - 1)], n2in)
            V.tensor_tensor(T.both[:, 0:Q], T.accin[:, (N - 2) * Q:(N - 1) * Q], T.accin[:, (N - 1) * Q:N * Q], A.add).then_inc(sem.vW, 1)
        elif c == "D":
            V.wait_ge(sem.vW, 1)
            V.wait_ge(sem.arb, nin)
            V.tensor_tensor(T.both[:, Q:], T.both[:, 0:Q], T.accin[:, N * Q:(N + 1) * Q], A.add).then_inc(sem.vW, 1)
        elif c == "E":
            ws = [x for x in FINAL if x[-1] == w][0]
            lo, hi = ws[0] * HQ, (w + 1) * HQ
            V.wait_ge(sem.vW, 2)
            V.wait_ge(sm("vt", w), N)
            V.tensor_tensor(T.res[:, lo:hi], T.term[:, (N - 1) * Q + lo:(N - 1) * Q + hi], T.both[:, Q + lo:Q + hi],
                            A.add).then_inc(sm("ve", w), 1)
        elif c == "G":
            i = VPIECE[w]
            lo, hi = pieces(n)[i]
            V.wait_ge(sm("sn", w) if s else sem.s0, max(s, 1))
            V.tensor_copy(T.kg[:, 16 * (n * H + lo):16 * (n * H + hi)],
                          T.kS[:].indirect(T.cu[:, n * H + lo:n * H + hi])).then_inc(sm("sg%d" % i, w), 1)
        elif c == "L":
            V.wait_ge(sm("va", w), s + 1)
            for b in range(B):
                k0 = 2 * (n + 1) * H - 1 - 32 * b
                V.tensor_scalar(T.rr[:, n * H + 16 * b:n * H + 16 * b + 16], T.m16[:], T.rmax[:, k0:k0 + 1], 0.0,
                                A.mult, A.max).then_inc(sm("vl", w), 1)
        elif c == "Y":
            V.wait_ge(sm("ps", w), s + 1)
            V.tensor_copy(wv(T.srep, n), T["pS%d" % (n % 2)][:, 0:H]).then_inc(sm("vy", w), 1)
        else:
            V.wait_ge(sm("vc", w), B * (s + 1))
            V.wait_ge(sm("vy", w), s + 1)
            if n >= 1:
                V.wait_ge(sm("vt", (n - 1) % W), (n - 1) // W + 1)
            V.tensor_tensor(T.term[:, n * HQ:n * HQ + H], T.kS[:].indirect(lst_out(n)), wv(T.srep, n), A.mult).then_inc(sm("vt", w), 1)

    V.wait_ge(sem.z0, 8)
    for n in range(2):
        vec("Z", n)
    V.wait_ge(sem.vE, 1)
    V.wait_ge(sem.ldnb, 16)
    for n in range(W):
        for e in range(2):
            V.tensor_scalar(T.cf[:, n, e, :], T.nbI[:].indirect(T.lin[:, B * n:B * n + B]), -2048.0, None, A.add).then_inc(sem.vF, 1)
    V.wait_ge(sem.arY, nin)
    for lo, hi in TABLE[0]:
        V.tensor_copy(T.nbbr[:, 16 * lo:16 * hi], T.nbI[:].indirect(T.brIn[:, lo:hi])).then_inc(sem.vnb, 1)
        if lo == 0:
            vec("X", 0)
    V.wait_ge(sem.ldk, 16)
    slots(VECTOR, lambda c, n: vec(c, n) if (c, n) not in (("Z", 0), ("Z", 1), ("X", 0)) else None)

    PE.wait_ge(sem.vI, 2)
    PE.wait_ge(sem.vX, 1)
    for i in range(2):
        pB, us = T["pB%d" % i], slice(4 * i, 4 * i + 4)
        PE.matmul(pB[:, 0:128:2], T.mE[:, 16:144], T.brT[:, us, 0, :], True, False)
        PE.matmul(pB[:, 0:128:2], T.mE[:, 0:128], T.brT[:, us, 1, :], False, True)
        PE.matmul(pB[:, 1:128:2], T.mO[:, 32:160], T.brT[:, us, 0, :], True, False)
        PE.matmul(pB[:, 1:128:2], T.mO[:, 16:144], T.brT[:, us, 1, :], False, True).then_inc(sem["pb%d" % i], 1)
    PE.wait_ge(sem.vC, 5)
    done = [0] * NW

    def ten(c, n):
        s, w = divmod(n, W)
        pU, pP, pS = T["pU%d" % (n % 2)], T["pP%d" % (n % 2)], T["pS%d" % (n % 2)]
        if c == "M":
            if n >= 2:
                PE.wait_ge(sm("vb", (n - 2) % W), (n - 2) // W + 1)
            PE.matmul(pU[:, 0:2 * H], T.par[:], T.half[:], True, False)
            PE.wait_ge(sm("vz", w), s + 1)
        elif c == "U":
            i = done[n]
            done[n] += 1
            PE.wait_ge(sm("sg%d" % i, w), s + 1)
            for t in range(pieces(n)[i][0] // 2, pieces(n)[i][1] // 2):
                lo = (n % 2) * ZW + 16 + 128 * t - 2 * (t % 8)
                mm = PE.matmul(pU[:, 32 * (t // 8):32 * (t // 8) + 32], T.zq[:, lo:lo + 128],
                               T.kg[:, n * 16 * H + 32 * t:n * 16 * H + 32 * t + 32], False, t == HQ // 2 - 1)
            if t == HQ // 2 - 1:
                mm.then_inc(sm("pu", w), 1)
        elif c == "P":
            PE.wait_ge(sm("vx", w), s + 1)
            if n >= 2:
                PE.wait_ge(sm("vc", (n - 2) % W), B * ((n - 2) // W + 1))
            PE.matmul(pP[:, 16:16 + 48 * B], T.c16[:], T.c1[:], True, False)
            for b, (plus, minus) in enumerate(((T.mE, T.gE), (T.mO, T.gO))):
                for h in range(2):
                    x, o = 16 + 16 * (b - h), 16 + 48 * b
                    PE.matmul(pP[:, o:o + 32], plus[:, x:x + 128], T.cT[:, 2 * n:2 * n + 2, h, :], False, False)
                    mm = PE.matmul(pP[:, o + 1:o + 33], minus[:, x:x + 128], T.cT[:, 2 * n:2 * n + 2, h, :], False, b + h == 2)
            mm.then_inc(sm("pp", w), 1)
        else:
            PE.wait_ge(sm("vl", w), B * (s + 1))
            PE.matmul(pS[:, 0:H], T.bo[:], wv(T.rr, n), True, True).then_inc(sm("ps", w), 1)

    slots(TENSOR, ten)

    piece = [0] * NW

    def sca(c, n):
        s, w = divmod(n, W)
        if c == "N":
            if n == W:
                table(*TABLE[2])
                SC.wait_ge(sem.vnb, 4)
            SC.wait_ge(sem["arl%d" % n], nin)
            SC.activation(wv(T.cu, n), T.nbbr[:].indirect(lst_in(n)), F.Copy).then_inc(sm("sn", w), 1)
        elif c == "F":
            if s >= 2:
                SC.wait_ge(sm("sf", w), 2 * (s - 1))
            for e in range(2):
                SC.activation(T.cf[:, n, e, :], T.nbbr[:].indirect(lst_in(n)), F.Identity, bias=neg).then_inc(sm("sf", w), 1)
        elif c == "L":
            SC.wait_ge(sm("va", w), s + 1)
            for b in range(B):
                k0 = 2 * (n + 1) * H - 1 - 32 * b
                SC.activation(T.rr[:, n * H + 16 * b:n * H + 16 * b + 16], T.m16[:], F.Relu,
                              scale=T.rmax[:, k0:k0 + 1]).then_inc(sm("vl", w), 1)
        elif c == "Y":
            SC.wait_ge(sm("ps", w), s + 1)
            SC.activation(wv(T.srep, n), T["pS%d" % (n % 2)][:, 0:H], F.Copy).then_inc(sm("vy", w), 1)
        else:
            i = piece[n]
            piece[n] += 1
            if i == VPIECE[w]:
                return
            if i == 0 and s >= 1:
                SC.wait_ge(sm("sn", w), s)
            if s >= 1:
                SC.wait_ge(sm("sg%d" % i, w), s)
            lo, hi = pieces(n)[i]
            SC.activation(T.kg[:, 16 * (n * H + lo):16 * (n * H + hi)], T.kS[:].indirect(T.cu[:, n * H + lo:n * H + hi]),
                          F.Copy).then_inc(sm("sg%d" % i, w), 1)

    def table(lo, hi):
        SC.activation(T.nbbr[:, 16 * lo:16 * hi], T.nbI[:].indirect(T.brIn[:, lo:hi]), F.Copy).then_inc(sem.vnb, 1)

    SC.wait_ge(sem.z0, 1)
    for i in range(1, 8):
        SC.activation(T.zq[:, i * ZW // 4:(i + 1) * ZW // 4], T.zq[:, 0:ZW // 4], F.Copy).then_inc(sem.z0, 1)
        if i == 4:
            SC.wait_ge(sem.pb0, 1)
            for U in range(4):
                SC.activation(T.brY[:, :, 2 * U:2 * U + 2], T.pB0[:, 32 * U:32 * U + 32], F.Identity, bias=pos).then_inc(sem.vY, 1)
    SC.wait_ge(sem.vE, 1)
    SC.wait_ge(sem.vI, 2)
    SC.wait_ge(sem.ldnb, 16)
    SC.activation(T.cu[:, 0:Q], T.nbI[:].indirect(T.lin[:, 0:B * W]), F.Copy).then_inc(sem.s0, 1)
    SC.wait_ge(sem.arY, nin)
    table(*TABLE[1])
    SC.wait_ge(sem.s0, 1)
    SC.wait_ge(sem.ldk, 16)
    slots(SCALAR, lambda c, n: sca(c, n) if c not in "NF" or n >= W else None)
